import numpy as np
import ml_dtypes


def mxq(x, axis, fmt="e4m3"):
    dtype, down = {"e4m3": (ml_dtypes.float8_e4m3fn, 7), "e5m2": (ml_dtypes.float8_e5m2, 14)}[fmt]
    v = np.moveaxis(np.asarray(x, np.float32).astype(ml_dtypes.bfloat16).astype(np.float64), axis, -1)
    blocks = v.reshape(v.shape[:-1] + (-1, 32))
    amax = np.abs(blocks).max(-1, keepdims=True)
    byte = np.maximum(np.where(amax > 0, np.frexp(amax)[1] - 1 + 127, 0) - down, 1)
    scale = np.exp2(byte - 127.0)
    codes = (blocks / scale).astype(np.float32).astype(dtype).astype(np.float64)
    return np.moveaxis((codes * scale).reshape(v.shape), -1, axis)


WIDE = False


def mx_kscale(k):
    if not WIDE:
        return np.ones(k)
    levels = np.array([10, -10, 5, -5, 0])
    if k % 512:
        return np.exp2(np.random.permutation(np.resize(levels, k // 32))).repeat(32)
    a = np.empty((k // 512, 16))
    for p in range(k // 512):
        a[p, :8] = np.random.permutation(np.resize(levels, 8))
        for g in range(8):
            far = levels[np.abs(levels - a[p, g]) >= 10]
            a[p, g + 8] = far[np.random.randint(len(far))]
    return np.exp2(a.ravel()).repeat(32)


def f64(x):
    return np.asarray(x).astype(np.float64)


def striped(idx):
    return np.tile(idx.reshape(-1, 16).T, (8, 1)).astype(np.uint16)


def unstriped(offs):
    return offs[:16].T.reshape(-1).astype(np.int64)


def pack_weight(w):
    k, n = w.shape
    w = f64(np.asarray(w, np.float32).astype(ml_dtypes.bfloat16)).reshape(k // 32, 32, n)
    amax = np.abs(w).max(1)
    byte = np.clip(np.where(amax > 0, np.frexp(amax)[1] - 1 + 127 - 7, 1), 1, 254)
    scaled = (w * np.exp2(127.0 - byte)[:, None, :]).reshape(k, n).astype(np.float32)
    words = np.ascontiguousarray(scaled.reshape(k // 512, 128, 4, n).transpose(0, 1, 3, 2)).astype(ml_dtypes.float8_e4m3fn).view(np.uint8)
    return words, np.ascontiguousarray(byte.astype(np.uint8).reshape(k // 512, 16, n))


def unpack_weight(words, scales):
    g, p, n, _ = words.shape
    vals = np.ascontiguousarray(words).view(ml_dtypes.float8_e4m3fn).astype(np.float64) * np.repeat(np.exp2(scales.astype(np.float64) - 127.0), 8, axis=1)[..., None]
    return vals.transpose(0, 1, 3, 2).reshape(g * 512, n)


def sigmoid(v):
    return 1.0 / (1.0 + np.exp(-np.maximum(v, -700.0)))


K, T, S, V, H, G = 512, 2048, 512, 512, 512, 1024


def setup_inputs():
    n = np.random.standard_normal
    s = mx_kscale(K)[:, None]
    u = mx_kscale(H)
    packed_xT = pack_weight(n((K, T)) * s)
    packed_pT = pack_weight(n((H, G)) / np.sqrt(4 * H) / u[:, None])
    packed_qT = pack_weight(n((H, G)) / np.sqrt(4 * H) / u[:, None])
    return {
        "x_words": packed_xT[0],
        "x_scales": packed_xT[1],
        "w1": (n((K, H)) / np.sqrt(K) / s * u).astype(np.float32),
        "w2": (n((K, H)) / np.sqrt(K) / s * u).astype(np.float32),
        "rr": (n((H, S))).astype(np.float32),
        "ri": (n((H, S))).astype(np.float32),
        "p_words": packed_pT[0],
        "p_scales": packed_pT[1],
        "q_words": packed_qT[0],
        "q_scales": packed_qT[1],
        "offs": striped(np.random.permutation(T)[:S]),
        "tail": striped(np.random.permutation(G)[:V]),
    }


def reference(x_words, x_scales, w1, w2, rr, ri, p_words, p_scales, q_words, q_scales, offs, tail):
    xq = unpack_weight(x_words, x_scales)[:, unstriped(offs)]
    y = mxq(f64(w1), 0, "e4m3").T @ xq
    z = y * f64(rr)
    p_tail = unpack_weight(p_words, p_scales)[:, unstriped(tail)]
    e = mxq(f64(w2), 0, "e4m3").T @ xq
    g = e * f64(ri)
    q_tail = unpack_weight(q_words, q_scales)[:, unstriped(tail)]
    s = mxq(z, 0, "e4m3").T @ p_tail + mxq(g, 0, "e4m3").T @ q_tail
    return sigmoid(s)

@@ -1,0 +1,158 @@
+from contextlib import ExitStack
+
+import concourse.mybir as mybir
+
+K, T, S, V, H, G = 512, 2048, 512, 512, 512, 1024
+FLOPS = 2 * 2 * K * H * S + 2 * 2 * H * S * V
+
+F32 = mybir.dt.float32
+BF16 = mybir.dt.bfloat16
+I32 = mybir.dt.int32
+U32 = mybir.dt.uint32
+U16 = mybir.dt.uint16
+U8 = mybir.dt.uint8
+FP8X4 = mybir.dt.float8_e4m3fn_x4
+MULT = mybir.AluOpType.mult
+SIGMOID = mybir.ActivationFunctionType.Sigmoid
+
+P = 128
+PACK = 4
+TQ = 128
+NQ = S // TQ
+
+
+def tile_picked_zcplx_simple_p_kernel(tc, x_words, x_scales, w1, w2, rr, ri, p_words, p_scales, q_words, q_scales, offs, tail, out):
+    nc = tc.nc
+    with ExitStack() as ctx:
+        keep = ctx.enter_context(tc.tile_pool(name="keep", bufs=1))
+        psum = ctx.enter_context(tc.psum_pool(name="psum", bufs=1))
+
+        def new(name, shape, dtype):
+            return keep.tile(shape, dtype, name=name, align_bytes=64)
+
+        offs_t = new("offs_t", [P, S // 16], U16)
+        tail_t = new("tail_t", [P, V // 16], U16)
+        nc.sync.dma_start(offs_t[:], offs)
+        nc.sync.dma_start(tail_t[:], tail)
+
+        def load_scales(name, scales, width, zero_engine, queue):
+            table = new(name, [P, width], U8)
+            zero_engine.memset(table[:].bitcast(I32), 0)
+            for q in range(4):
+                queue.dma_start(table[32 * q : 32 * q + 4, :].bitcast(I32), scales[0, 4 * q : 4 * q + 4, :].bitcast(I32))
+            return table
+
+        def load_words(name, words, width):
+            table = new(name, [P, width], I32)
+            nc.sync.dma_start(table[:], words[0].rearrange("p n t -> p (n t)").bitcast(I32))
+            return table
+
+        def load_rows(name, src, c0, c1):
+            raw = new(name, [P, PACK, c1 - c0], F32)
+            nc.sync.dma_start(raw[:], src.rearrange("(p j) c -> p j c", j=PACK)[:, :, c0:c1])
+            return raw
+
+        xs_tab = load_scales("xs_tab", x_scales, T, nc.vector, nc.scalar)
+        warm = new("warm", [P, 1], F32)
+        nc.vector.memset(warm[:], 0.0)
+        warm_out = new("warm_out", [P, 1], F32)
+        nc.scalar.activation(warm_out[:], warm[:], SIGMOID)
+        ps_tab = load_scales("ps_tab", p_scales, G, nc.gpsimd, nc.gpsimd)
+        qs_tab = load_scales("qs_tab", q_scales, G, nc.gpsimd, nc.gpsimd)
+
+        w1_raw = [load_rows("w1_raw", w1, 0, H)]
+        xw_tab = load_words("xw_tab", x_words, T)
+        pw_tab = load_words("pw_tab", p_words, G)
+        rr_raw = [load_rows("rr_raw", rr, 0, S)]
+        w2_raw = [load_rows("w2_raw%d" % h, w2, h * H // 2, (h + 1) * H // 2) for h in range(2)]
+        qw_tab = load_words("qw_tab", q_words, G)
+        ri_raw = [load_rows("ri_raw%d" % h, ri, h * S // 2, (h + 1) * S // 2) for h in range(2)]
+
+        def gather_words(name, table, offsets):
+            picked = new(name, [P, S], U32)
+            nc.vector.tensor_copy(picked[:], table[:].bitcast(U32).indirect(offsets[:]))
+            return picked
+
+        def gather_scales(name, table, offsets):
+            picked = new(name, [P, S], U8)
+            nc.vector.tensor_copy(picked[:], table[:].indirect(offsets[:]))
+            return picked
+
+        def cast_weight(name, pieces):
+            grouped = new(name, [P, PACK * H], BF16)
+            view = grouped[:].rearrange("p (t m j) -> p m j t", t=PACK, j=PACK)
+            mw = P // len(pieces)
+            for h, raw in enumerate(pieces):
+                nc.scalar.copy(view[:, h * mw : (h + 1) * mw, :, :], raw[:].rearrange("p j (m t) -> p m j t", t=PACK))
+            return grouped
+
+        def quantize(name, grouped, width):
+            codes = new(name + "_codes", [P, width], U32)
+            scales = new(name + "_scales", [P, width], U8)
+            nc.vector.quantize_mx(out=codes[:].bitcast(FP8X4), scales=scales[:], in_=grouped)
+            return codes, scales
+
+        def project(name, wq, c):
+            bank = psum.tile([P, PACK, TQ], F32, name=name, tag=name, bufs=2)
+            cols = slice(c * TQ, (c + 1) * TQ)
+            for j in range(PACK):
+                wc = slice(j * P, (j + 1) * P)
+                nc.tensor.matmul_mx(out=bank[:, j, :], lhsT=wq[0][:, wc].bitcast(FP8X4), lhsT_scale=wq[1][:, wc],
+                                    rhs=xw[:, cols].bitcast(FP8X4), rhs_scale=xs[:, cols], start=True, stop=True)
+            return bank
+
+        def product(dst, bank, pieces, c):
+            per = NQ // len(pieces)
+            raw = pieces[c // per]
+            c0 = (c % per) * TQ
+            nc.vector.tensor_tensor(
+                dst.rearrange("p (c i j) -> p c j i", i=2, j=PACK),
+                bank[:].rearrange("p j (c i) -> p c j i", i=2),
+                raw[:, :, c0 : c0 + TQ].rearrange("p j (c i) -> p c j i", i=2),
+                MULT,
+            )
+
+        w1_bf = cast_weight("w1_bf", w1_raw)
+        w2_bf = cast_weight("w2_bf", w2_raw)
+
+        xs = gather_scales("xs", xs_tab, offs_t)
+        ps = gather_scales("ps", ps_tab, tail_t)
+        qs = gather_scales("qs", qs_tab, tail_t)
+        xw = gather_words("xw", xw_tab, offs_t)
+        w1q = quantize("w1q", w1_bf[:], H)
+        pw = gather_words("pw", pw_tab, tail_t)
+
+        z_bf = [new("z_bf%d" % h, [P, 2 * TQ * PACK], BF16) for h in range(2)]
+        zq = []
+        for c in range(NQ):
+            bank = project("ybank", w1q, c)
+            product(z_bf[c // 2][:, (c % 2) * TQ * PACK : (c % 2 + 1) * TQ * PACK], bank, rr_raw, c)
+        for h in range(2):
+            zq.append(quantize("zq%d" % h, z_bf[h][:], 2 * TQ))
+        sbank = []
+        for c in range(NQ):
+            bank = psum.tile([P, V], F32, name="sbank%d" % c, tag="sbank%d" % c)
+            cols = slice((c % 2) * TQ, (c % 2 + 1) * TQ)
+            nc.tensor.matmul_mx(out=bank[:], lhsT=zq[c // 2][0][:, cols].bitcast(FP8X4), lhsT_scale=zq[c // 2][1][:, cols],
+                                rhs=pw[:].bitcast(FP8X4), rhs_scale=ps[:], start=True, stop=False)
+            sbank.append(bank)
+
+        w2q = quantize("w2q", w2_bf[:], H)
+        qw = gather_words("qw", qw_tab, tail_t)
+
+        g_bf = [new("g_bf%d" % c, [P, TQ * PACK], BF16) for c in range(NQ)]
+
+        def finish(c):
+            gq = quantize("gq%d" % c, g_bf[c][:], TQ)
+            nc.tensor.matmul_mx(out=sbank[c][:], lhsT=gq[0][:].bitcast(FP8X4), lhsT_scale=gq[1][:],
+                                rhs=qw[:].bitcast(FP8X4), rhs_scale=qs[:], start=False, stop=True)
+            res = new("res%d" % c, [P, V], F32)
+            nc.scalar.activation(res[:], sbank[c][:], SIGMOID)
+            nc.sync.dma_start(out[c * TQ : (c + 1) * TQ, :], res[:])
+
+        for c in range(NQ):
+            bank = project("ebank", w2q, c)
+            product(g_bf[c][:], bank, ri_raw, c)
+            if c > 0:
+                finish(c - 1)
+        finish(NQ - 1)

@@ -27,20 +27,12 @@ def tile_picked_zcplx_simple_p_kernel(tc, x_words, x_scales, w1, w2, rr, ri, p_w
         keep = ctx.enter_context(tc.tile_pool(name="keep", bufs=1))
         psum = ctx.enter_context(tc.psum_pool(name="psum", bufs=1))
 
-        def new(name, shape, dtype):
-            return keep.tile(shape, dtype, name=name, align_bytes=64)
+        def new(name, shape, dtype, tag=None):
+            return keep.tile(shape, dtype, name=name, tag=tag or name, align_bytes=64)
 
-        offs_t = new("offs_t", [P, S // 16], U16)
-        tail_t = new("tail_t", [P, V // 16], U16)
-        nc.sync.dma_start(offs_t[:], offs)
-        nc.sync.dma_start(tail_t[:], tail)
-
-        def load_scales(name, scales, width, zero_engine, queue):
-            table = new(name, [P, width], U8)
-            zero_engine.memset(table[:].bitcast(I32), 0)
+        def load_scales(table, scales):
             for q in range(4):
-                queue.dma_start(table[32 * q : 32 * q + 4, :].bitcast(I32), scales[0, 4 * q : 4 * q + 4, :].bitcast(I32))
-            return table
+                nc.sync.dma_start(table[32 * q : 32 * q + 4, :].bitcast(I32), scales[0, 4 * q : 4 * q + 4, :].bitcast(I32))
 
         def load_words(name, words, width):
             table = new(name, [P, width], I32)
@@ -52,20 +44,35 @@ def tile_picked_zcplx_simple_p_kernel(tc, x_words, x_scales, w1, w2, rr, ri, p_w
             nc.sync.dma_start(raw[:], src.rearrange("(p j) c -> p j c", j=PACK)[:, :, c0:c1])
             return raw
 
-        xs_tab = load_scales("xs_tab", x_scales, T, nc.vector, nc.scalar)
+        def zeroed(name, width, engine):
+            table = new(name, [P, width], U8)
+            engine.memset(table[:].bitcast(I32), 0)
+            return table
+
+        def load_list(name, src):
+            tile = new(name, [P, S // 16], U16)
+            nc.sync.dma_start(tile[:], src)
+            return tile
+
+        ps_tab = zeroed("ps_tab", G, nc.vector)
+        xs_tab = zeroed("xs_tab", T, nc.vector)
+        qs_tab = zeroed("qs_tab", G, nc.vector)
         warm = new("warm", [P, 1], F32)
-        nc.vector.memset(warm[:], 0.0)
+        nc.gpsimd.memset(warm[:], 0.0)
         warm_out = new("warm_out", [P, 1], F32)
         nc.scalar.activation(warm_out[:], warm[:], SIGMOID)
-        ps_tab = load_scales("ps_tab", p_scales, G, nc.gpsimd, nc.gpsimd)
-        qs_tab = load_scales("qs_tab", q_scales, G, nc.gpsimd, nc.gpsimd)
 
-        w1_raw = [load_rows("w1_raw", w1, 0, H)]
-        xw_tab = load_words("xw_tab", x_words, T)
         pw_tab = load_words("pw_tab", p_words, G)
+        tail_t = load_list("tail_t", tail)
+        load_scales(ps_tab, p_scales)
+        qw_tab = load_words("qw_tab", q_words, G)
+        w1_raw = [load_rows("w1_raw", w1, 0, H)]
+        offs_t = load_list("offs_t", offs)
+        load_scales(xs_tab, x_scales)
+        xw_tab = load_words("xw_tab", x_words, T)
+        load_scales(qs_tab, q_scales)
         rr_raw = [load_rows("rr_raw", rr, 0, S)]
         w2_raw = [load_rows("w2_raw%d" % h, w2, h * H // 2, (h + 1) * H // 2) for h in range(2)]
-        qw_tab = load_words("qw_tab", q_words, G)
         ri_raw = [load_rows("ri_raw%d" % h, ri, h * S // 2, (h + 1) * S // 2) for h in range(2)]
 
         def gather_words(name, table, offsets):
@@ -73,8 +80,8 @@ def tile_picked_zcplx_simple_p_kernel(tc, x_words, x_scales, w1, w2, rr, ri, p_w
             nc.vector.tensor_copy(picked[:], table[:].bitcast(U32).indirect(offsets[:]))
             return picked
 
-        def gather_scales(name, table, offsets):
-            picked = new(name, [P, S], U8)
+        def gather_scales(name, table, offsets, tag=None):
+            picked = new(name, [P, S], U8, tag)
             nc.vector.tensor_copy(picked[:], table[:].indirect(offsets[:]))
             return picked
 
@@ -86,14 +93,14 @@ def tile_picked_zcplx_simple_p_kernel(tc, x_words, x_scales, w1, w2, rr, ri, p_w
                 nc.scalar.copy(view[:, h * mw : (h + 1) * mw, :, :], raw[:].rearrange("p j (m t) -> p m j t", t=PACK))
             return grouped
 
-        def quantize(name, grouped, width):
-            codes = new(name + "_codes", [P, width], U32)
+        def quantize(name, grouped, width, tag=None):
+            codes = new(name + "_codes", [P, width], U32, tag)
             scales = new(name + "_scales", [P, width], U8)
             nc.vector.quantize_mx(out=codes[:].bitcast(FP8X4), scales=scales[:], in_=grouped)
             return codes, scales
 
         def project(name, wq, c):
-            bank = psum.tile([P, PACK, TQ], F32, name=name, tag=name, bufs=2)
+            bank = psum.tile([P, PACK, TQ], F32, name="%s%d" % (name, c), tag="%s%d" % (name, c))
             cols = slice(c * TQ, (c + 1) * TQ)
             for j in range(PACK):
                 wc = slice(j * P, (j + 1) * P)
@@ -115,30 +122,28 @@ def tile_picked_zcplx_simple_p_kernel(tc, x_words, x_scales, w1, w2, rr, ri, p_w
         w1_bf = cast_weight("w1_bf", w1_raw)
         w2_bf = cast_weight("w2_bf", w2_raw)
 
-        xs = gather_scales("xs", xs_tab, offs_t)
-        ps = gather_scales("ps", ps_tab, tail_t)
-        qs = gather_scales("qs", qs_tab, tail_t)
-        xw = gather_words("xw", xw_tab, offs_t)
-        w1q = quantize("w1q", w1_bf[:], H)
         pw = gather_words("pw", pw_tab, tail_t)
+        ps = gather_scales("ps", ps_tab, tail_t)
+        qw = gather_words("qw", qw_tab, tail_t)
+        xs = gather_scales("xs", xs_tab, offs_t)
+        w1q = quantize("w1q", w1_bf[:], H, "xs_tab")
+        xw = gather_words("xw", xw_tab, offs_t)
+        qs = gather_scales("qs", qs_tab, tail_t, "w1_bf")
 
-        z_bf = [new("z_bf%d" % h, [P, 2 * TQ * PACK], BF16) for h in range(2)]
-        zq = []
+        z_bf = new("z_bf", [P, S * PACK], BF16)
         for c in range(NQ):
             bank = project("ybank", w1q, c)
-            product(z_bf[c // 2][:, (c % 2) * TQ * PACK : (c % 2 + 1) * TQ * PACK], bank, rr_raw, c)
-        for h in range(2):
-            zq.append(quantize("zq%d" % h, z_bf[h][:], 2 * TQ))
+            product(z_bf[:, c * TQ * PACK : (c + 1) * TQ * PACK], bank, rr_raw, c)
+        w2q = quantize("w2q", w2_bf[:], H)
+        ebank = [project("ebank", w2q, c) for c in range(NQ)]
+        zq = quantize("zq", z_bf[:], S, "w2_bf")
         sbank = []
         for c in range(NQ):
-            bank = psum.tile([P, V], F32, name="sbank%d" % c, tag="sbank%d" % c)
-            cols = slice((c % 2) * TQ, (c % 2 + 1) * TQ)
-            nc.tensor.matmul_mx(out=bank[:], lhsT=zq[c // 2][0][:, cols].bitcast(FP8X4), lhsT_scale=zq[c // 2][1][:, cols],
+            bank = psum.tile([P, V], F32, name="sbank%d" % c, tag="ybank%d" % c)
+            cols = slice(c * TQ, (c + 1) * TQ)
+            nc.tensor.matmul_mx(out=bank[:], lhsT=zq[0][:, cols].bitcast(FP8X4), lhsT_scale=zq[1][:, cols],
                                 rhs=pw[:].bitcast(FP8X4), rhs_scale=ps[:], start=True, stop=False)
             sbank.append(bank)
-
-        w2q = quantize("w2q", w2_bf[:], H)
-        qw = gather_words("qw", qw_tab, tail_t)
 
         g_bf = [new("g_bf%d" % c, [P, TQ * PACK], BF16) for c in range(NQ)]
 
@@ -151,8 +156,7 @@ def tile_picked_zcplx_simple_p_kernel(tc, x_words, x_scales, w1, w2, rr, ri, p_w
             nc.sync.dma_start(out[c * TQ : (c + 1) * TQ, :], res[:])
 
         for c in range(NQ):
-            bank = project("ebank", w2q, c)
-            product(g_bf[c][:], bank, ri_raw, c)
+            product(g_bf[c][:], ebank[c], ri_raw, c)
             if c > 0:
                 finish(c - 1)
         finish(NQ - 1)

@@ -19,6 +19,7 @@ P = 128
 PACK = 4
 TQ = 128
 NQ = S // TQ
+P_ROW, Q_ROW = 4, 8
 
 
 def tile_picked_zcplx_simple_p_kernel(tc, x_words, x_scales, w1, w2, rr, ri, p_words, p_scales, q_words, q_scales, offs, tail, out):
@@ -30,9 +31,9 @@ def tile_picked_zcplx_simple_p_kernel(tc, x_words, x_scales, w1, w2, rr, ri, p_w
         def new(name, shape, dtype, tag=None):
             return keep.tile(shape, dtype, name=name, tag=tag or name, align_bytes=64)
 
-        def load_scales(table, scales):
-            for q in range(4):
-                nc.sync.dma_start(table[32 * q : 32 * q + 4, :].bitcast(I32), scales[0, 4 * q : 4 * q + 4, :].bitcast(I32))
+        def load_scales(table, scales, first):
+            for r in range(4):
+                nc.sync.dma_start(table[first + r : P : 32, :].bitcast(I32), scales[0, r:16:4, :].bitcast(I32))
 
         def load_words(name, words, width):
             table = new(name, [P, width], I32)
@@ -64,13 +65,13 @@ def tile_picked_zcplx_simple_p_kernel(tc, x_words, x_scales, w1, w2, rr, ri, p_w
 
         pw_tab = load_words("pw_tab", p_words, G)
         tail_t = load_list("tail_t", tail)
-        load_scales(ps_tab, p_scales)
+        load_scales(ps_tab, p_scales, P_ROW)
         qw_tab = load_words("qw_tab", q_words, G)
         w1_raw = [load_rows("w1_raw", w1, 0, H)]
         offs_t = load_list("offs_t", offs)
-        load_scales(xs_tab, x_scales)
+        load_scales(xs_tab, x_scales, 0)
         xw_tab = load_words("xw_tab", x_words, T)
-        load_scales(qs_tab, q_scales)
+        load_scales(qs_tab, q_scales, Q_ROW)
         rr_raw = [load_rows("rr_raw", rr, 0, S)]
         w2_raw = [load_rows("w2_raw%d" % h, w2, h * H // 2, (h + 1) * H // 2) for h in range(2)]
         ri_raw = [load_rows("ri_raw%d" % h, ri, h * S // 2, (h + 1) * S // 2) for h in range(2)]
@@ -142,7 +143,7 @@ def tile_picked_zcplx_simple_p_kernel(tc, x_words, x_scales, w1, w2, rr, ri, p_w
             bank = psum.tile([P, V], F32, name="sbank%d" % c, tag="ybank%d" % c)
             cols = slice(c * TQ, (c + 1) * TQ)
             nc.tensor.matmul_mx(out=bank[:], lhsT=zq[0][:, cols].bitcast(FP8X4), lhsT_scale=zq[1][:, cols],
-                                rhs=pw[:].bitcast(FP8X4), rhs_scale=ps[:], start=True, stop=False)
+                                rhs=pw[:].bitcast(FP8X4), rhs_scale=ps[P_ROW:P, :], start=True, stop=False)
             sbank.append(bank)
 
         g_bf = [new("g_bf%d" % c, [P, TQ * PACK], BF16) for c in range(NQ)]
@@ -150,10 +151,13 @@ def tile_picked_zcplx_simple_p_kernel(tc, x_words, x_scales, w1, w2, rr, ri, p_w
         def finish(c):
             gq = quantize("gq%d" % c, g_bf[c][:], TQ)
             nc.tensor.matmul_mx(out=sbank[c][:], lhsT=gq[0][:].bitcast(FP8X4), lhsT_scale=gq[1][:],
-                                rhs=qw[:].bitcast(FP8X4), rhs_scale=qs[:], start=False, stop=True)
-            res = new("res%d" % c, [P, V], F32)
-            nc.scalar.activation(res[:], sbank[c][:], SIGMOID)
-            nc.sync.dma_start(out[c * TQ : (c + 1) * TQ, :], res[:])
+                                rhs=qw[:].bitcast(FP8X4), rhs_scale=qs[Q_ROW:P, :], start=False, stop=True)
+            parts = 2 if c == NQ - 1 else 1
+            for h in range(parts):
+                cols = slice(h * V // parts, (h + 1) * V // parts)
+                res = new("res%d_%d" % (c, h), [P, V // parts], F32)
+                nc.scalar.activation(res[:], sbank[c][:, cols], SIGMOID)
+                nc.sync.dma_start(out[c * TQ : (c + 1) * TQ, cols], res[:])
 
         for c in range(NQ):
             product(g_bf[c][:], ebank[c], ri_raw, c)

@@ -131,20 +131,29 @@ def tile_picked_zcplx_simple_p_kernel(tc, x_words, x_scales, w1, w2, rr, ri, p_w
         xw = gather_words("xw", xw_tab, offs_t)
         qs = gather_scales("qs", qs_tab, tail_t, "w1_bf")
 
-        z_bf = new("z_bf", [P, S * PACK], BF16)
-        for c in range(NQ):
-            bank = project("ybank", w1q, c)
-            product(z_bf[:, c * TQ * PACK : (c + 1) * TQ * PACK], bank, rr_raw, c)
+        ybank = [project("ybank", w1q, c) for c in range(NQ)]
+        z_bf = [new("z_bf%d" % h, [P, 2 * TQ * PACK], BF16) for h in range(2)]
+        sbank = []
+
+        def z_products(h):
+            for u in range(2):
+                product(z_bf[h][:, u * TQ * PACK : (u + 1) * TQ * PACK], ybank[2 * h + u], rr_raw, 2 * h + u)
+
+        def open_scores(h, tag=None):
+            zq = quantize("zq%d" % h, z_bf[h][:], 2 * TQ, tag)
+            for u in range(2):
+                bank = psum.tile([P, V], F32, name="sbank%d" % (2 * h + u), tag="ybank%d" % (2 * h + u))
+                cols = slice(u * TQ, (u + 1) * TQ)
+                nc.tensor.matmul_mx(out=bank[:], lhsT=zq[0][:, cols].bitcast(FP8X4), lhsT_scale=zq[1][:, cols],
+                                    rhs=pw[:].bitcast(FP8X4), rhs_scale=ps[P_ROW:P, :], start=True, stop=False)
+                sbank.append(bank)
+
+        z_products(0)
+        open_scores(0)
+        z_products(1)
         w2q = quantize("w2q", w2_bf[:], H)
         ebank = [project("ebank", w2q, c) for c in range(NQ)]
-        zq = quantize("zq", z_bf[:], S, "w2_bf")
-        sbank = []
-        for c in range(NQ):
-            bank = psum.tile([P, V], F32, name="sbank%d" % c, tag="ybank%d" % c)
-            cols = slice(c * TQ, (c + 1) * TQ)
-            nc.tensor.matmul_mx(out=bank[:], lhsT=zq[0][:, cols].bitcast(FP8X4), lhsT_scale=zq[1][:, cols],
-                                rhs=pw[:].bitcast(FP8X4), rhs_scale=ps[P_ROW:P, :], start=True, stop=False)
-            sbank.append(bank)
+        open_scores(1, "w2_bf")
 
         g_bf = [new("g_bf%d" % c, [P, TQ * PACK], BF16) for c in range(NQ)]
 

@@ -13,13 +13,16 @@ U16 = mybir.dt.uint16
 U8 = mybir.dt.uint8
 FP8X4 = mybir.dt.float8_e4m3fn_x4
 MULT = mybir.AluOpType.mult
+ADD = mybir.AluOpType.add
 SIGMOID = mybir.ActivationFunctionType.Sigmoid
 
 P = 128
 PACK = 4
 TQ = 128
 NQ = S // TQ
-P_ROW, Q_ROW = 4, 8
+P_ROW = 4
+ROWS = 16
+M_SCALAR = 88
 
 
 def tile_picked_zcplx_simple_p_kernel(tc, x_words, x_scales, w1, w2, rr, ri, p_words, p_scales, q_words, q_scales, offs, tail, out):
@@ -62,18 +65,19 @@ def tile_picked_zcplx_simple_p_kernel(tc, x_words, x_scales, w1, w2, rr, ri, p_w
         nc.gpsimd.memset(warm[:], 0.0)
         warm_out = new("warm_out", [P, 1], F32)
         nc.scalar.activation(warm_out[:], warm[:], SIGMOID)
+        qs = zeroed("qs", V, nc.gpsimd)
 
         pw_tab = load_words("pw_tab", p_words, G)
         tail_t = load_list("tail_t", tail)
         load_scales(ps_tab, p_scales, P_ROW)
         qw_tab = load_words("qw_tab", q_words, G)
-        w1_raw = [load_rows("w1_raw", w1, 0, H)]
+        w1_raw = load_rows("w1_raw", w1, 0, H)
         offs_t = load_list("offs_t", offs)
         load_scales(xs_tab, x_scales, 0)
         xw_tab = load_words("xw_tab", x_words, T)
-        load_scales(qs_tab, q_scales, Q_ROW)
-        rr_raw = [load_rows("rr_raw", rr, 0, S)]
-        w2_raw = [load_rows("w2_raw%d" % h, w2, h * H // 2, (h + 1) * H // 2) for h in range(2)]
+        nc.sync.dma_start(qs_tab[0:ROWS, :].bitcast(I32), q_scales[0].bitcast(I32))
+        w2_raw = load_rows("w2_raw", w2, 0, H)
+        rr_raw = [load_rows("rr_raw%d" % h, rr, h * S // 2, (h + 1) * S // 2) for h in range(2)]
         ri_raw = [load_rows("ri_raw%d" % h, ri, h * S // 2, (h + 1) * S // 2) for h in range(2)]
 
         def gather_words(name, table, offsets):
@@ -86,12 +90,15 @@ def tile_picked_zcplx_simple_p_kernel(tc, x_words, x_scales, w1, w2, rr, ri, p_w
             nc.vector.tensor_copy(picked[:], table[:].indirect(offsets[:]))
             return picked
 
-        def cast_weight(name, pieces):
+        def cast_weight(name, raw, m_scalar):
             grouped = new(name, [P, PACK * H], BF16)
-            view = grouped[:].rearrange("p (t m j) -> p m j t", t=PACK, j=PACK)
-            mw = P // len(pieces)
-            for h, raw in enumerate(pieces):
-                nc.scalar.copy(view[:, h * mw : (h + 1) * mw, :, :], raw[:].rearrange("p j (m t) -> p m j t", t=PACK))
+            dst = grouped[:].rearrange("p (t m j) -> p m j t", t=PACK, j=PACK)
+            src = raw[:].rearrange("p j (m t) -> p m j t", t=PACK)
+            nc.scalar.copy(dst[:, 0:m_scalar, :, :], src[:, 0:m_scalar, :, :])
+            if m_scalar < P:
+                dst = grouped[:].rearrange("p (t m j) -> p m t j", t=PACK, j=PACK)
+                src = raw[:].rearrange("p j (m t) -> p m t j", t=PACK)
+                nc.gpsimd.tensor_scalar(dst[:, m_scalar:P, :, :], src[:, m_scalar:P, :, :], 1.0, 0.0, MULT, ADD)
             return grouped
 
         def quantize(name, grouped, width, tag=None):
@@ -120,8 +127,8 @@ def tile_picked_zcplx_simple_p_kernel(tc, x_words, x_scales, w1, w2, rr, ri, p_w
                 MULT,
             )
 
-        w1_bf = cast_weight("w1_bf", w1_raw)
-        w2_bf = cast_weight("w2_bf", w2_raw)
+        w1_bf = cast_weight("w1_bf", w1_raw, M_SCALAR)
+        w2_bf = cast_weight("w2_bf", w2_raw, P)
 
         pw = gather_words("pw", pw_tab, tail_t)
         ps = gather_scales("ps", ps_tab, tail_t)
@@ -129,7 +136,9 @@ def tile_picked_zcplx_simple_p_kernel(tc, x_words, x_scales, w1, w2, rr, ri, p_w
         xs = gather_scales("xs", xs_tab, offs_t)
         w1q = quantize("w1q", w1_bf[:], H, "xs_tab")
         xw = gather_words("xw", xw_tab, offs_t)
-        qs = gather_scales("qs", qs_tab, tail_t, "w1_bf")
+        qs_rows = gather_scales("qs_rows", qs_tab, tail_t, "w1_bf")
+        for quad in range(4):
+            nc.sync.dma_start(qs[32 * quad : 32 * quad + 4, :].bitcast(I32), qs_rows[4 * quad : 4 * quad + 4, :].bitcast(I32))
 
         ybank = [project("ybank", w1q, c) for c in range(NQ)]
         z_bf = [new("z_bf%d" % h, [P, 2 * TQ * PACK], BF16) for h in range(2)]
@@ -149,24 +158,25 @@ def tile_picked_zcplx_simple_p_kernel(tc, x_words, x_scales, w1, w2, rr, ri, p_w
                 sbank.append(bank)
 
         z_products(0)
-        open_scores(0)
-        z_products(1)
         w2q = quantize("w2q", w2_bf[:], H)
         ebank = [project("ebank", w2q, c) for c in range(NQ)]
-        open_scores(1, "w2_bf")
+        open_scores(0)
+        z_products(1)
+        open_scores(1)
 
         g_bf = [new("g_bf%d" % c, [P, TQ * PACK], BF16) for c in range(NQ)]
 
         def finish(c):
             gq = quantize("gq%d" % c, g_bf[c][:], TQ)
             nc.tensor.matmul_mx(out=sbank[c][:], lhsT=gq[0][:].bitcast(FP8X4), lhsT_scale=gq[1][:],
-                                rhs=qw[:].bitcast(FP8X4), rhs_scale=qs[Q_ROW:P, :], start=False, stop=True)
+                                rhs=qw[:].bitcast(FP8X4), rhs_scale=qs[:], start=False, stop=True)
             parts = 2 if c == NQ - 1 else 1
             for h in range(parts):
                 cols = slice(h * V // parts, (h + 1) * V // parts)
                 res = new("res%d_%d" % (c, h), [P, V // parts], F32)
                 nc.scalar.activation(res[:], sbank[c][:, cols], SIGMOID)
-                nc.sync.dma_start(out[c * TQ : (c + 1) * TQ, cols], res[:])
+                queue = nc.scalar if (c, h) == (NQ - 1, parts - 1) else nc.sync
+                queue.dma_start(out[c * TQ : (c + 1) * TQ, cols], res[:])
 
         for c in range(NQ):
             product(g_bf[c][:], ebank[c], ri_raw, c)

@@ -76,8 +76,10 @@ def tile_picked_zcplx_simple_p_kernel(tc, x_words, x_scales, w1, w2, rr, ri, p_w
         load_scales(xs_tab, x_scales, 0)
         xw_tab = load_words("xw_tab", x_words, T)
         nc.sync.dma_start(qs_tab[0:ROWS, :].bitcast(I32), q_scales[0].bitcast(I32))
-        w2_raw = load_rows("w2_raw", w2, 0, H)
-        rr_raw = [load_rows("rr_raw%d" % h, rr, h * S // 2, (h + 1) * S // 2) for h in range(2)]
+        w2_raw, rr_raw = [], []
+        for h in range(2):
+            w2_raw.append(load_rows("w2_raw%d" % h, w2, h * H // 2, (h + 1) * H // 2))
+            rr_raw.append(load_rows("rr_raw%d" % h, rr, h * S // 2, (h + 1) * S // 2))
         ri_raw = [load_rows("ri_raw%d" % h, ri, h * S // 2, (h + 1) * S // 2) for h in range(2)]
 
         def gather_words(name, table, offsets):
@@ -128,7 +130,10 @@ def tile_picked_zcplx_simple_p_kernel(tc, x_words, x_scales, w1, w2, rr, ri, p_w
             )
 
         w1_bf = cast_weight("w1_bf", w1_raw, M_SCALAR)
-        w2_bf = cast_weight("w2_bf", w2_raw, P)
+        w2_bf = new("w2_bf", [P, PACK * H], BF16)
+        for h in range(2):
+            nc.scalar.copy(w2_bf[:].rearrange("p (t m j) -> p m j t", t=PACK, j=PACK)[:, h * P // 2 : (h + 1) * P // 2, :, :],
+                           w2_raw[h][:].rearrange("p j (m t) -> p m j t", t=PACK))
 
         pw = gather_words("pw", pw_tab, tail_t)
         ps = gather_scales("ps", ps_tab, tail_t)
@@ -158,9 +163,9 @@ def tile_picked_zcplx_simple_p_kernel(tc, x_words, x_scales, w1, w2, rr, ri, p_w
                 sbank.append(bank)
 
         z_products(0)
+        open_scores(0)
         w2q = quantize("w2q", w2_bf[:], H)
         ebank = [project("ebank", w2q, c) for c in range(NQ)]
-        open_scores(0)
         z_products(1)
         open_scores(1)
 

@@ -23,6 +23,7 @@ NQ = S // TQ
 P_ROW = 4
 ROWS = 16
 M_SCALAR = 88
+W2_CUTS = (0, 320, H)
 
 
 def tile_picked_zcplx_simple_p_kernel(tc, x_words, x_scales, w1, w2, rr, ri, p_words, p_scales, q_words, q_scales, offs, tail, out):
@@ -78,7 +79,7 @@ def tile_picked_zcplx_simple_p_kernel(tc, x_words, x_scales, w1, w2, rr, ri, p_w
         nc.sync.dma_start(qs_tab[0:ROWS, :].bitcast(I32), q_scales[0].bitcast(I32))
         w2_raw, rr_raw = [], []
         for h in range(2):
-            w2_raw.append(load_rows("w2_raw%d" % h, w2, h * H // 2, (h + 1) * H // 2))
+            w2_raw.append(load_rows("w2_raw%d" % h, w2, W2_CUTS[h], W2_CUTS[h + 1]))
             rr_raw.append(load_rows("rr_raw%d" % h, rr, h * S // 2, (h + 1) * S // 2))
         ri_raw = [load_rows("ri_raw%d" % h, ri, h * S // 2, (h + 1) * S // 2) for h in range(2)]
 
@@ -132,7 +133,7 @@ def tile_picked_zcplx_simple_p_kernel(tc, x_words, x_scales, w1, w2, rr, ri, p_w
         w1_bf = cast_weight("w1_bf", w1_raw, M_SCALAR)
         w2_bf = new("w2_bf", [P, PACK * H], BF16)
         for h in range(2):
-            nc.scalar.copy(w2_bf[:].rearrange("p (t m j) -> p m j t", t=PACK, j=PACK)[:, h * P // 2 : (h + 1) * P // 2, :, :],
+            nc.scalar.copy(w2_bf[:].rearrange("p (t m j) -> p m j t", t=PACK, j=PACK)[:, W2_CUTS[h] // PACK : W2_CUTS[h + 1] // PACK, :, :],
                            w2_raw[h][:].rearrange("p j (m t) -> p m j t", t=PACK))
 
         pw = gather_words("pw", pw_tab, tail_t)
@@ -147,44 +148,48 @@ def tile_picked_zcplx_simple_p_kernel(tc, x_words, x_scales, w1, w2, rr, ri, p_w
 
         ybank = [project("ybank", w1q, c) for c in range(NQ)]
         z_bf = [new("z_bf%d" % h, [P, 2 * TQ * PACK], BF16) for h in range(2)]
-        sbank = []
+        sbank = [[] for _ in range(NQ)]
+        zq = []
 
         def z_products(h):
             for u in range(2):
                 product(z_bf[h][:, u * TQ * PACK : (u + 1) * TQ * PACK], ybank[2 * h + u], rr_raw, 2 * h + u)
 
-        def open_scores(h, tag=None):
-            zq = quantize("zq%d" % h, z_bf[h][:], 2 * TQ, tag)
-            for u in range(2):
-                bank = psum.tile([P, V], F32, name="sbank%d" % (2 * h + u), tag="ybank%d" % (2 * h + u))
-                cols = slice(u * TQ, (u + 1) * TQ)
-                nc.tensor.matmul_mx(out=bank[:], lhsT=zq[0][:, cols].bitcast(FP8X4), lhsT_scale=zq[1][:, cols],
-                                    rhs=pw[:].bitcast(FP8X4), rhs_scale=ps[P_ROW:P, :], start=True, stop=False)
-                sbank.append(bank)
+        def open_scores(c, v0, v1, tag):
+            bank = psum.tile([P, v1 - v0], F32, name="sbank%d_%d" % (c, v0), tag=tag)
+            codes, scales = zq[c // 2]
+            cols = slice((c % 2) * TQ, (c % 2 + 1) * TQ)
+            nc.tensor.matmul_mx(out=bank[:], lhsT=codes[:, cols].bitcast(FP8X4), lhsT_scale=scales[:, cols],
+                                rhs=pw[:, v0:v1].bitcast(FP8X4), rhs_scale=ps[P_ROW:P, v0:v1], start=True, stop=False)
+            sbank[c].append((bank, v0, v1))
 
         z_products(0)
-        open_scores(0)
+        zq.append(quantize("zq0", z_bf[0][:], 2 * TQ))
+        open_scores(0, 0, V, "ybank0")
+        open_scores(1, 0, V, "ybank1")
         w2q = quantize("w2q", w2_bf[:], H)
         ebank = [project("ebank", w2q, c) for c in range(NQ)]
         z_products(1)
-        open_scores(1)
+        zq.append(quantize("zq1", z_bf[1][:], 2 * TQ))
+        open_scores(2, 0, V, "ybank2")
+        open_scores(3, 0, V // 2, "ybank3")
 
         g_bf = [new("g_bf%d" % c, [P, TQ * PACK], BF16) for c in range(NQ)]
 
         def finish(c):
             gq = quantize("gq%d" % c, g_bf[c][:], TQ)
-            nc.tensor.matmul_mx(out=sbank[c][:], lhsT=gq[0][:].bitcast(FP8X4), lhsT_scale=gq[1][:],
-                                rhs=qw[:].bitcast(FP8X4), rhs_scale=qs[:], start=False, stop=True)
-            parts = 2 if c == NQ - 1 else 1
-            for h in range(parts):
-                cols = slice(h * V // parts, (h + 1) * V // parts)
-                res = new("res%d_%d" % (c, h), [P, V // parts], F32)
-                nc.scalar.activation(res[:], sbank[c][:, cols], SIGMOID)
-                queue = nc.scalar if (c, h) == (NQ - 1, parts - 1) else nc.sync
-                queue.dma_start(out[c * TQ : (c + 1) * TQ, cols], res[:])
+            for bank, v0, v1 in sbank[c]:
+                nc.tensor.matmul_mx(out=bank[:], lhsT=gq[0][:].bitcast(FP8X4), lhsT_scale=gq[1][:],
+                                    rhs=qw[:, v0:v1].bitcast(FP8X4), rhs_scale=qs[:, v0:v1], start=False, stop=True)
+                res = new("res%d_%d" % (c, v0), [P, v1 - v0], F32)
+                nc.scalar.activation(res[:], bank[:], SIGMOID)
+                queue = nc.scalar if (c, v1) == (NQ - 1, V) else nc.sync
+                queue.dma_start(out[c * TQ : (c + 1) * TQ, v0:v1], res[:])
 
         for c in range(NQ):
             product(g_bf[c][:], ebank[c], ri_raw, c)
-            if c > 0:
+            if c == 0:
+                open_scores(3, V // 2, V, "ebank0")
+            else:
                 finish(c - 1)
         finish(NQ - 1)

@@ -119,14 +119,14 @@ def tile_picked_zcplx_simple_p_kernel(tc, x_words, x_scales, w1, w2, rr, ri, p_w
                                     rhs=xw[:, cols].bitcast(FP8X4), rhs_scale=xs[:, cols], start=True, stop=True)
             return bank
 
-        def product(dst, bank, pieces, c):
+        def product(dst, bank, pieces, c, t0=0, t1=TQ):
             per = NQ // len(pieces)
             raw = pieces[c // per]
             c0 = (c % per) * TQ
             nc.vector.tensor_tensor(
-                dst.rearrange("p (c i j) -> p c j i", i=2, j=PACK),
-                bank[:].rearrange("p j (c i) -> p c j i", i=2),
-                raw[:, :, c0 : c0 + TQ].rearrange("p j (c i) -> p c j i", i=2),
+                dst[:, t0 * PACK : t1 * PACK].rearrange("p (c i j) -> p c j i", i=2, j=PACK),
+                bank[:, :, t0:t1].rearrange("p j (c i) -> p c j i", i=2),
+                raw[:, :, c0 + t0 : c0 + t1].rearrange("p j (c i) -> p c j i", i=2),
                 MULT,
             )
 
@@ -147,34 +147,18 @@ def tile_picked_zcplx_simple_p_kernel(tc, x_words, x_scales, w1, w2, rr, ri, p_w
             nc.sync.dma_start(qs[32 * quad : 32 * quad + 4, :].bitcast(I32), qs_rows[4 * quad : 4 * quad + 4, :].bitcast(I32))
 
         ybank = [project("ybank", w1q, c) for c in range(NQ)]
-        z_bf = [new("z_bf%d" % h, [P, 2 * TQ * PACK], BF16) for h in range(2)]
+        z_bf = [new("z_bf%d" % c, [P, TQ * PACK], BF16) for c in range(NQ)]
+        g_bf = [new("g_bf%d" % c, [P, TQ * PACK], BF16) for c in range(NQ)]
         sbank = [[] for _ in range(NQ)]
-        zq = []
-
-        def z_products(h):
-            for u in range(2):
-                product(z_bf[h][:, u * TQ * PACK : (u + 1) * TQ * PACK], ybank[2 * h + u], rr_raw, 2 * h + u)
+        zq = {}
 
         def open_scores(c, v0, v1, tag):
+            if c not in zq:
+                zq[c] = quantize("zq%d" % c, z_bf[c][:], TQ)
             bank = psum.tile([P, v1 - v0], F32, name="sbank%d_%d" % (c, v0), tag=tag)
-            codes, scales = zq[c // 2]
-            cols = slice((c % 2) * TQ, (c % 2 + 1) * TQ)
-            nc.tensor.matmul_mx(out=bank[:], lhsT=codes[:, cols].bitcast(FP8X4), lhsT_scale=scales[:, cols],
+            nc.tensor.matmul_mx(out=bank[:], lhsT=zq[c][0][:].bitcast(FP8X4), lhsT_scale=zq[c][1][:],
                                 rhs=pw[:, v0:v1].bitcast(FP8X4), rhs_scale=ps[P_ROW:P, v0:v1], start=True, stop=False)
             sbank[c].append((bank, v0, v1))
-
-        z_products(0)
-        zq.append(quantize("zq0", z_bf[0][:], 2 * TQ))
-        open_scores(0, 0, V, "ybank0")
-        open_scores(1, 0, V, "ybank1")
-        w2q = quantize("w2q", w2_bf[:], H)
-        ebank = [project("ebank", w2q, c) for c in range(NQ)]
-        z_products(1)
-        zq.append(quantize("zq1", z_bf[1][:], 2 * TQ))
-        open_scores(2, 0, V, "ybank2")
-        open_scores(3, 0, V // 2, "ybank3")
-
-        g_bf = [new("g_bf%d" % c, [P, TQ * PACK], BF16) for c in range(NQ)]
 
         def finish(c):
             gq = quantize("gq%d" % c, g_bf[c][:], TQ)
@@ -186,10 +170,22 @@ def tile_picked_zcplx_simple_p_kernel(tc, x_words, x_scales, w1, w2, rr, ri, p_w
                 queue = nc.scalar if (c, v1) == (NQ - 1, V) else nc.sync
                 queue.dma_start(out[c * TQ : (c + 1) * TQ, v0:v1], res[:])
 
-        for c in range(NQ):
+        product(z_bf[0][:], ybank[0], rr_raw, 0)
+        product(z_bf[1][:], ybank[1], rr_raw, 1)
+        open_scores(0, 0, V, "ybank0")
+        w2q = quantize("w2q", w2_bf[:], H)
+        open_scores(1, 0, V, "ybank1")
+        ebank = [project("ebank", w2q, c) for c in range(NQ)]
+        product(z_bf[2][:], ybank[2], rr_raw, 2)
+        product(z_bf[3][:], ybank[3], rr_raw, 3)
+        open_scores(2, 0, V, "ybank2")
+        product(g_bf[0][:], ebank[0], ri_raw, 0)
+        open_scores(3, 0, V // 2, "ybank3")
+        open_scores(3, V // 2, V, "ebank0")
+        for c in range(1, NQ - 1):
             product(g_bf[c][:], ebank[c], ri_raw, c)
-            if c == 0:
-                open_scores(3, V // 2, V, "ebank0")
-            else:
-                finish(c - 1)
-        finish(NQ - 1)
+            finish(c - 1)
+        product(g_bf[3][:], ebank[3], ri_raw, 3, 0, TQ // 2)
+        finish(2)
+        product(g_bf[3][:], ebank[3], ri_raw, 3, TQ // 2, TQ)
+        finish(3)

@@ -24,6 +24,7 @@ P_ROW = 4
 ROWS = 16
 M_SCALAR = 88
 W2_CUTS = (0, 320, H)
+W2_SCALAR_END = 416
 
 
 def tile_picked_zcplx_simple_p_kernel(tc, x_words, x_scales, w1, w2, rr, ri, p_words, p_scales, q_words, q_scales, offs, tail, out):
@@ -132,9 +133,13 @@ def tile_picked_zcplx_simple_p_kernel(tc, x_words, x_scales, w1, w2, rr, ri, p_w
 
         w1_bf = cast_weight("w1_bf", w1_raw, M_SCALAR)
         w2_bf = new("w2_bf", [P, PACK * H], BF16)
-        for h in range(2):
-            nc.scalar.copy(w2_bf[:].rearrange("p (t m j) -> p m j t", t=PACK, j=PACK)[:, W2_CUTS[h] // PACK : W2_CUTS[h + 1] // PACK, :, :],
-                           w2_raw[h][:].rearrange("p j (m t) -> p m j t", t=PACK))
+
+        def w2_cast_views(h, c0, c1):
+            dst = w2_bf[:].rearrange("p (t m j) -> p m j t", t=PACK, j=PACK)[:, c0 // PACK : c1 // PACK, :, :]
+            return dst, w2_raw[h][:, :, c0 - W2_CUTS[h] : c1 - W2_CUTS[h]].rearrange("p j (m t) -> p m j t", t=PACK)
+
+        nc.scalar.copy(*w2_cast_views(0, 0, W2_CUTS[1]))
+        nc.scalar.copy(*w2_cast_views(1, W2_CUTS[1], W2_SCALAR_END))
 
         pw = gather_words("pw", pw_tab, tail_t)
         ps = gather_scales("ps", ps_tab, tail_t)
@@ -172,6 +177,7 @@ def tile_picked_zcplx_simple_p_kernel(tc, x_words, x_scales, w1, w2, rr, ri, p_w
 
         product(z_bf[0][:], ybank[0], rr_raw, 0)
         product(z_bf[1][:], ybank[1], rr_raw, 1)
+        nc.vector.tensor_copy(*w2_cast_views(1, W2_SCALAR_END, H))
         open_scores(0, 0, V, "ybank0")
         w2q = quantize("w2q", w2_bf[:], H)
         open_scores(1, 0, V, "ybank1")

@@ -67,7 +67,6 @@ def tile_picked_zcplx_simple_p_kernel(tc, x_words, x_scales, w1, w2, rr, ri, p_w
         nc.gpsimd.memset(warm[:], 0.0)
         warm_out = new("warm_out", [P, 1], F32)
         nc.scalar.activation(warm_out[:], warm[:], SIGMOID)
-        qs = zeroed("qs", V, nc.gpsimd)
 
         pw_tab = load_words("pw_tab", p_words, G)
         tail_t = load_list("tail_t", tail)
@@ -148,8 +147,9 @@ def tile_picked_zcplx_simple_p_kernel(tc, x_words, x_scales, w1, w2, rr, ri, p_w
         w1q = quantize("w1q", w1_bf[:], H, "xs_tab")
         xw = gather_words("xw", xw_tab, offs_t)
         qs_rows = gather_scales("qs_rows", qs_tab, tail_t, "w1_bf")
+        qs = new("qs", [P, V], U8, "w2_raw0")
         for quad in range(4):
-            nc.sync.dma_start(qs[32 * quad : 32 * quad + 4, :].bitcast(I32), qs_rows[4 * quad : 4 * quad + 4, :].bitcast(I32))
+            nc.scalar.dma_start(qs[32 * quad : 32 * quad + 32, :].bitcast(I32), qs_rows[4 * quad : 4 * quad + 32, :].bitcast(I32))
 
         ybank = [project("ybank", w1q, c) for c in range(NQ)]
         z_bf = [new("z_bf%d" % c, [P, TQ * PACK], BF16) for c in range(NQ)]

@@ -20,9 +20,11 @@ P = 128
 PACK = 4
 TQ = 128
 NQ = S // TQ
-P_ROW = 4
-ROWS = 16
-M_SCALAR = 88
+QUAD = 32
+SPREAD = 8
+X_ROW = 4
+PQ_ROW = 12
+W1_SCALAR = 88
 W2_CUTS = (0, 320, H)
 W2_SCALAR_END = 416
 
@@ -36,17 +38,16 @@ def tile_picked_zcplx_simple_p_kernel(tc, x_words, x_scales, w1, w2, rr, ri, p_w
         def new(name, shape, dtype, tag=None):
             return keep.tile(shape, dtype, name=name, tag=tag or name, align_bytes=64)
 
-        def load_scales(table, scales, first):
-            for r in range(4):
-                nc.sync.dma_start(table[first + r : P : 32, :].bitcast(I32), scales[0, r:16:4, :].bitcast(I32))
+        def load_scales(table, scales):
+            nc.sync.dma_start(table[0:P:SPREAD, :].bitcast(I32), scales[0].bitcast(I32))
 
         def load_words(name, words, width):
             table = new(name, [P, width], I32)
             nc.sync.dma_start(table[:], words[0].rearrange("p n t -> p (n t)").bitcast(I32))
             return table
 
-        def load_rows(name, src, c0, c1):
-            raw = new(name, [P, PACK, c1 - c0], F32)
+        def load_rows(name, src, c0, c1, tag=None):
+            raw = new(name, [P, PACK, c1 - c0], F32, tag)
             nc.sync.dma_start(raw[:], src.rearrange("(p j) c -> p j c", j=PACK)[:, :, c0:c1])
             return raw
 
@@ -60,49 +61,39 @@ def tile_picked_zcplx_simple_p_kernel(tc, x_words, x_scales, w1, w2, rr, ri, p_w
             nc.sync.dma_start(tile[:], src)
             return tile
 
-        ps_tab = zeroed("ps_tab", G, nc.vector)
+        def place_rows(plane, rows, first):
+            for r in range(4):
+                nc.sync.dma_start(plane[first + r : P : QUAD, :].bitcast(I32), rows[SPREAD * r : P : QUAD, :].bitcast(I32))
+
         xs_tab = zeroed("xs_tab", T, nc.vector)
+        ps_tab = zeroed("ps_tab", G, nc.gpsimd)
         qs_tab = zeroed("qs_tab", G, nc.vector)
         warm = new("warm", [P, 1], F32)
         nc.gpsimd.memset(warm[:], 0.0)
         warm_out = new("warm_out", [P, 1], F32)
         nc.scalar.activation(warm_out[:], warm[:], SIGMOID)
+        xs = zeroed("xs", S, nc.gpsimd)
+        pqs = zeroed("pqs", 2 * V, nc.gpsimd)
 
         pw_tab = load_words("pw_tab", p_words, G)
-        tail_t = load_list("tail_t", tail)
-        load_scales(ps_tab, p_scales, P_ROW)
-        qw_tab = load_words("qw_tab", q_words, G)
-        w1_raw = load_rows("w1_raw", w1, 0, H)
         offs_t = load_list("offs_t", offs)
-        load_scales(xs_tab, x_scales, 0)
+        load_scales(xs_tab, x_scales)
+        load_scales(ps_tab, p_scales)
+        tail_t = load_list("tail_t", tail)
+        load_scales(qs_tab, q_scales)
+        w1_raw = load_rows("w1_raw", w1, 0, H)
         xw_tab = load_words("xw_tab", x_words, T)
-        nc.sync.dma_start(qs_tab[0:ROWS, :].bitcast(I32), q_scales[0].bitcast(I32))
-        w2_raw, rr_raw = [], []
-        for h in range(2):
-            w2_raw.append(load_rows("w2_raw%d" % h, w2, W2_CUTS[h], W2_CUTS[h + 1]))
-            rr_raw.append(load_rows("rr_raw%d" % h, rr, h * S // 2, (h + 1) * S // 2))
-        ri_raw = [load_rows("ri_raw%d" % h, ri, h * S // 2, (h + 1) * S // 2) for h in range(2)]
+        qw_tab = load_words("qw_tab", q_words, G)
 
-        def gather_words(name, table, offsets):
-            picked = new(name, [P, S], U32)
+        def gather_words(name, table, offsets, tag=None):
+            picked = new(name, [P, S], U32, tag)
             nc.vector.tensor_copy(picked[:], table[:].bitcast(U32).indirect(offsets[:]))
             return picked
 
-        def gather_scales(name, table, offsets, tag=None):
-            picked = new(name, [P, S], U8, tag)
-            nc.vector.tensor_copy(picked[:], table[:].indirect(offsets[:]))
-            return picked
-
-        def cast_weight(name, raw, m_scalar):
-            grouped = new(name, [P, PACK * H], BF16)
-            dst = grouped[:].rearrange("p (t m j) -> p m j t", t=PACK, j=PACK)
-            src = raw[:].rearrange("p j (m t) -> p m j t", t=PACK)
-            nc.scalar.copy(dst[:, 0:m_scalar, :, :], src[:, 0:m_scalar, :, :])
-            if m_scalar < P:
-                dst = grouped[:].rearrange("p (t m j) -> p m t j", t=PACK, j=PACK)
-                src = raw[:].rearrange("p j (m t) -> p m t j", t=PACK)
-                nc.gpsimd.tensor_scalar(dst[:, m_scalar:P, :, :], src[:, m_scalar:P, :, :], 1.0, 0.0, MULT, ADD)
-            return grouped
+        def cast_views(grouped, raw, m0, m1, order):
+            dst = grouped[:].rearrange("p (t m j) -> p m %s" % order, t=PACK, j=PACK)
+            src = raw[:].rearrange("p j (m t) -> p m %s" % order, t=PACK)
+            return dst[:, m0:m1, :, :], src[:, m0:m1, :, :]
 
         def quantize(name, grouped, width, tag=None):
             codes = new(name + "_codes", [P, width], U32, tag)
@@ -110,13 +101,13 @@ def tile_picked_zcplx_simple_p_kernel(tc, x_words, x_scales, w1, w2, rr, ri, p_w
             nc.vector.quantize_mx(out=codes[:].bitcast(FP8X4), scales=scales[:], in_=grouped)
             return codes, scales
 
-        def project(name, wq, c):
-            bank = psum.tile([P, PACK, TQ], F32, name="%s%d" % (name, c), tag="%s%d" % (name, c))
+        def project(name, wq, c, tag):
+            bank = psum.tile([P, PACK, TQ], F32, name="%s%d" % (name, c), tag=tag)
             cols = slice(c * TQ, (c + 1) * TQ)
             for j in range(PACK):
                 wc = slice(j * P, (j + 1) * P)
                 nc.tensor.matmul_mx(out=bank[:, j, :], lhsT=wq[0][:, wc].bitcast(FP8X4), lhsT_scale=wq[1][:, wc],
-                                    rhs=xw[:, cols].bitcast(FP8X4), rhs_scale=xs[:, cols], start=True, stop=True)
+                                    rhs=xw[:, cols].bitcast(FP8X4), rhs_scale=xs[X_ROW:P, cols], start=True, stop=True)
             return bank
 
         def product(dst, bank, pieces, c, t0=0, t1=TQ):
@@ -130,28 +121,30 @@ def tile_picked_zcplx_simple_p_kernel(tc, x_words, x_scales, w1, w2, rr, ri, p_w
                 MULT,
             )
 
-        w1_bf = cast_weight("w1_bf", w1_raw, M_SCALAR)
-        w2_bf = new("w2_bf", [P, PACK * H], BF16)
-
-        def w2_cast_views(h, c0, c1):
-            dst = w2_bf[:].rearrange("p (t m j) -> p m j t", t=PACK, j=PACK)[:, c0 // PACK : c1 // PACK, :, :]
-            return dst, w2_raw[h][:, :, c0 - W2_CUTS[h] : c1 - W2_CUTS[h]].rearrange("p j (m t) -> p m j t", t=PACK)
-
-        nc.scalar.copy(*w2_cast_views(0, 0, W2_CUTS[1]))
-        nc.scalar.copy(*w2_cast_views(1, W2_CUTS[1], W2_SCALAR_END))
-
+        xs_rows = new("xs_rows", [P, S], U8)
+        nc.vector.tensor_copy(xs_rows[:], xs_tab[:].indirect(offs_t[:]))
+        place_rows(xs, xs_rows, X_ROW)
+        pq_rows = new("pq_rows", [P, 2 * V], U8)
+        nc.vector.tensor_copy(pq_rows[:, 0:V], ps_tab[:].indirect(tail_t[:]))
+        w2_raw = [load_rows("w2_raw0", w2, 0, W2_CUTS[1], "ps_tab")]
         pw = gather_words("pw", pw_tab, tail_t)
-        ps = gather_scales("ps", ps_tab, tail_t)
-        qw = gather_words("qw", qw_tab, tail_t)
-        xs = gather_scales("xs", xs_tab, offs_t)
-        w1q = quantize("w1q", w1_bf[:], H, "xs_tab")
-        xw = gather_words("xw", xw_tab, offs_t)
-        qs_rows = gather_scales("qs_rows", qs_tab, tail_t, "w1_bf")
-        qs = new("qs", [P, V], U8, "w2_raw0")
-        for quad in range(4):
-            nc.scalar.dma_start(qs[32 * quad : 32 * quad + 32, :].bitcast(I32), qs_rows[4 * quad : 4 * quad + 32, :].bitcast(I32))
+        rr_raw = [load_rows("rr_raw0", rr, 0, S // 2, "pw_tab")]
+        nc.vector.tensor_copy(pq_rows[:, V : 2 * V], qs_tab[:].indirect(tail_t[:]))
+        w2_raw.append(load_rows("w2_raw1", w2, W2_CUTS[1], H, "qs_tab"))
+        place_rows(pqs, pq_rows, PQ_ROW)
 
-        ybank = [project("ybank", w1q, c) for c in range(NQ)]
+        w1_bf = new("w1_bf", [P, PACK * H], BF16)
+        nc.scalar.copy(*cast_views(w1_bf, w1_raw, 0, W1_SCALAR, "j t"))
+        nc.gpsimd.tensor_scalar(*cast_views(w1_bf, w1_raw, W1_SCALAR, P, "t j"), 1.0, 0.0, MULT, ADD)
+        w1q = quantize("w1q", w1_bf[:], H)
+        xw = gather_words("xw", xw_tab, offs_t)
+
+        rr_raw.append(load_rows("rr_raw1", rr, S // 2, S, "w1_raw"))
+        ri_raw = [load_rows("ri_raw0", ri, 0, S // 2, "w1_bf")]
+
+        ybank = [project("ybank", w1q, c, "ybank%d" % c) for c in range(2)]
+        qw = gather_words("qw", qw_tab, tail_t, "xw_tab")
+        ri_raw.append(load_rows("ri_raw1", ri, S // 2, S, "qw_tab"))
         z_bf = [new("z_bf%d" % c, [P, TQ * PACK], BF16) for c in range(NQ)]
         g_bf = [new("g_bf%d" % c, [P, TQ * PACK], BF16) for c in range(NQ)]
         sbank = [[] for _ in range(NQ)]
@@ -162,31 +155,40 @@ def tile_picked_zcplx_simple_p_kernel(tc, x_words, x_scales, w1, w2, rr, ri, p_w
                 zq[c] = quantize("zq%d" % c, z_bf[c][:], TQ)
             bank = psum.tile([P, v1 - v0], F32, name="sbank%d_%d" % (c, v0), tag=tag)
             nc.tensor.matmul_mx(out=bank[:], lhsT=zq[c][0][:].bitcast(FP8X4), lhsT_scale=zq[c][1][:],
-                                rhs=pw[:, v0:v1].bitcast(FP8X4), rhs_scale=ps[P_ROW:P, v0:v1], start=True, stop=False)
+                                rhs=pw[:, v0:v1].bitcast(FP8X4), rhs_scale=pqs[PQ_ROW:P, v0:v1], start=True, stop=False)
             sbank[c].append((bank, v0, v1))
 
         def finish(c):
             gq = quantize("gq%d" % c, g_bf[c][:], TQ)
             for bank, v0, v1 in sbank[c]:
                 nc.tensor.matmul_mx(out=bank[:], lhsT=gq[0][:].bitcast(FP8X4), lhsT_scale=gq[1][:],
-                                    rhs=qw[:, v0:v1].bitcast(FP8X4), rhs_scale=qs[:, v0:v1], start=False, stop=True)
+                                    rhs=qw[:, v0:v1].bitcast(FP8X4), rhs_scale=pqs[PQ_ROW:P, V + v0 : V + v1], start=False, stop=True)
                 res = new("res%d_%d" % (c, v0), [P, v1 - v0], F32)
                 nc.scalar.activation(res[:], bank[:], SIGMOID)
                 queue = nc.scalar if (c, v1) == (NQ - 1, V) else nc.sync
                 queue.dma_start(out[c * TQ : (c + 1) * TQ, v0:v1], res[:])
 
-        product(z_bf[0][:], ybank[0], rr_raw, 0)
-        product(z_bf[1][:], ybank[1], rr_raw, 1)
+        w2_bf = new("w2_bf", [P, PACK * H], BF16)
+
+        def w2_cast_views(h, c0, c1):
+            dst = w2_bf[:].rearrange("p (t m j) -> p m j t", t=PACK, j=PACK)[:, c0 // PACK : c1 // PACK, :, :]
+            return dst, w2_raw[h][:, :, c0 - W2_CUTS[h] : c1 - W2_CUTS[h]].rearrange("p j (m t) -> p m j t", t=PACK)
+
+        nc.scalar.copy(*w2_cast_views(0, 0, W2_CUTS[1]))
+        nc.scalar.copy(*w2_cast_views(1, W2_CUTS[1], W2_SCALAR_END))
+        for c in range(2):
+            product(z_bf[c][:], ybank[c], rr_raw, c)
+            ybank.append(project("ybank", w1q, c + 2, "ybank%d" % c))
+        open_scores(0, 0, V, "sbank0")
         nc.vector.tensor_copy(*w2_cast_views(1, W2_SCALAR_END, H))
-        open_scores(0, 0, V, "ybank0")
+        open_scores(1, 0, V, "sbank1")
         w2q = quantize("w2q", w2_bf[:], H)
-        open_scores(1, 0, V, "ybank1")
-        ebank = [project("ebank", w2q, c) for c in range(NQ)]
+        ebank = [project("ebank", w2q, c, "ebank%d" % c) for c in range(NQ)]
         product(z_bf[2][:], ybank[2], rr_raw, 2)
         product(z_bf[3][:], ybank[3], rr_raw, 3)
-        open_scores(2, 0, V, "ybank2")
+        open_scores(2, 0, V, "ybank0")
         product(g_bf[0][:], ebank[0], ri_raw, 0)
-        open_scores(3, 0, V // 2, "ybank3")
+        open_scores(3, 0, V // 2, "ybank1")
         open_scores(3, V // 2, V, "ebank0")
         for c in range(1, NQ - 1):
             product(g_bf[c][:], ebank[c], ri_raw, c)

@@ -24,7 +24,6 @@ QUAD = 32
 SPREAD = 8
 X_ROW = 4
 PQ_ROW = 12
-W1_SCALAR = 88
 W2_CUTS = (0, 320, H)
 W2_SCALAR_END = 416
 
@@ -134,8 +133,7 @@ def tile_picked_zcplx_simple_p_kernel(tc, x_words, x_scales, w1, w2, rr, ri, p_w
         place_rows(pqs, pq_rows, PQ_ROW)
 
         w1_bf = new("w1_bf", [P, PACK * H], BF16)
-        nc.scalar.copy(*cast_views(w1_bf, w1_raw, 0, W1_SCALAR, "j t"))
-        nc.gpsimd.tensor_scalar(*cast_views(w1_bf, w1_raw, W1_SCALAR, P, "t j"), 1.0, 0.0, MULT, ADD)
+        nc.scalar.copy(*cast_views(w1_bf, w1_raw, 0, P, "j t"))
         w1q = quantize("w1q", w1_bf[:], H)
         xw = gather_words("xw", xw_tab, offs_t)
 

@@ -24,8 +24,8 @@ QUAD = 32
 SPREAD = 8
 X_ROW = 4
 PQ_ROW = 12
-W2_CUTS = (0, 320, H)
-W2_SCALAR_END = 416
+W2_CUTS = (0, 256, H)
+W2_SCALAR_END = 352
 
 
 def tile_picked_zcplx_simple_p_kernel(tc, x_words, x_scales, w1, w2, rr, ri, p_words, p_scales, q_words, q_scales, offs, tail, out):
@@ -64,8 +64,8 @@ def tile_picked_zcplx_simple_p_kernel(tc, x_words, x_scales, w1, w2, rr, ri, p_w
             for r in range(4):
                 nc.sync.dma_start(plane[first + r : P : QUAD, :].bitcast(I32), rows[SPREAD * r : P : QUAD, :].bitcast(I32))
 
-        xs_tab = zeroed("xs_tab", T, nc.vector)
-        ps_tab = zeroed("ps_tab", G, nc.gpsimd)
+        xs_tab = zeroed("xs_tab", T, nc.gpsimd)
+        ps_tab = zeroed("ps_tab", G, nc.vector)
         qs_tab = zeroed("qs_tab", G, nc.vector)
         warm = new("warm", [P, 1], F32)
         nc.gpsimd.memset(warm[:], 0.0)
@@ -74,13 +74,17 @@ def tile_picked_zcplx_simple_p_kernel(tc, x_words, x_scales, w1, w2, rr, ri, p_w
         xs = zeroed("xs", S, nc.gpsimd)
         pqs = zeroed("pqs", 2 * V, nc.gpsimd)
 
-        pw_tab = load_words("pw_tab", p_words, G)
+        w1_raw = new("w1_raw", [P, PACK, H], F32)
+        w1_rows = w1.rearrange("(p j) c -> p j c", j=PACK)
+        nc.sync.dma_start(w1_raw[:, 0:1, :], w1_rows[:, 0:1, :])
         offs_t = load_list("offs_t", offs)
         load_scales(xs_tab, x_scales)
-        load_scales(ps_tab, p_scales)
+        nc.sync.dma_start(w1_raw[:, 1:2, :], w1_rows[:, 1:2, :])
         tail_t = load_list("tail_t", tail)
+        load_scales(ps_tab, p_scales)
         load_scales(qs_tab, q_scales)
-        w1_raw = load_rows("w1_raw", w1, 0, H)
+        nc.sync.dma_start(w1_raw[:, 2:PACK, :], w1_rows[:, 2:PACK, :])
+        pw_tab = load_words("pw_tab", p_words, G)
         xw_tab = load_words("xw_tab", x_words, T)
         qw_tab = load_words("qw_tab", q_words, G)
 
@@ -123,14 +127,14 @@ def tile_picked_zcplx_simple_p_kernel(tc, x_words, x_scales, w1, w2, rr, ri, p_w
         xs_rows = new("xs_rows", [P, S], U8)
         nc.vector.tensor_copy(xs_rows[:], xs_tab[:].indirect(offs_t[:]))
         place_rows(xs, xs_rows, X_ROW)
+        rr_raw = [load_rows("rr_raw0", rr, 0, S // 2, "xs_tab")]
         pq_rows = new("pq_rows", [P, 2 * V], U8)
         nc.vector.tensor_copy(pq_rows[:, 0:V], ps_tab[:].indirect(tail_t[:]))
         w2_raw = [load_rows("w2_raw0", w2, 0, W2_CUTS[1], "ps_tab")]
-        pw = gather_words("pw", pw_tab, tail_t)
-        rr_raw = [load_rows("rr_raw0", rr, 0, S // 2, "pw_tab")]
         nc.vector.tensor_copy(pq_rows[:, V : 2 * V], qs_tab[:].indirect(tail_t[:]))
         w2_raw.append(load_rows("w2_raw1", w2, W2_CUTS[1], H, "qs_tab"))
         place_rows(pqs, pq_rows, PQ_ROW)
+        pw = gather_words("pw", pw_tab, tail_t)
 
         w1_bf = new("w1_bf", [P, PACK * H], BF16)
         nc.scalar.copy(*cast_views(w1_bf, w1_raw, 0, P, "j t"))

@@ -24,8 +24,6 @@ QUAD = 32
 SPREAD = 8
 X_ROW = 4
 PQ_ROW = 12
-W2_CUTS = (0, 256, H)
-W2_SCALAR_END = 352
 
 
 def tile_picked_zcplx_simple_p_kernel(tc, x_words, x_scales, w1, w2, rr, ri, p_words, p_scales, q_words, q_scales, offs, tail, out):
@@ -40,8 +38,8 @@ def tile_picked_zcplx_simple_p_kernel(tc, x_words, x_scales, w1, w2, rr, ri, p_w
         def load_scales(table, scales):
             nc.sync.dma_start(table[0:P:SPREAD, :].bitcast(I32), scales[0].bitcast(I32))
 
-        def load_words(name, words, width):
-            table = new(name, [P, width], I32)
+        def load_words(name, words, width, tag=None):
+            table = new(name, [P, width], I32, tag)
             nc.sync.dma_start(table[:], words[0].rearrange("p n t -> p (n t)").bitcast(I32))
             return table
 
@@ -76,17 +74,15 @@ def tile_picked_zcplx_simple_p_kernel(tc, x_words, x_scales, w1, w2, rr, ri, p_w
 
         w1_raw = new("w1_raw", [P, PACK, H], F32)
         w1_rows = w1.rearrange("(p j) c -> p j c", j=PACK)
-        nc.sync.dma_start(w1_raw[:, 0:1, :], w1_rows[:, 0:1, :])
+        nc.sync.dma_start(w1_raw[:, 0:2, :], w1_rows[:, 0:2, :])
         offs_t = load_list("offs_t", offs)
         load_scales(xs_tab, x_scales)
-        nc.sync.dma_start(w1_raw[:, 1:2, :], w1_rows[:, 1:2, :])
         tail_t = load_list("tail_t", tail)
         load_scales(ps_tab, p_scales)
         load_scales(qs_tab, q_scales)
         nc.sync.dma_start(w1_raw[:, 2:PACK, :], w1_rows[:, 2:PACK, :])
+        w2_raw = load_rows("w2_raw", w2, 0, H)
         pw_tab = load_words("pw_tab", p_words, G)
-        xw_tab = load_words("xw_tab", x_words, T)
-        qw_tab = load_words("qw_tab", q_words, G)
 
         def gather_words(name, table, offsets, tag=None):
             picked = new(name, [P, S], U32, tag)
@@ -127,26 +123,29 @@ def tile_picked_zcplx_simple_p_kernel(tc, x_words, x_scales, w1, w2, rr, ri, p_w
         xs_rows = new("xs_rows", [P, S], U8)
         nc.vector.tensor_copy(xs_rows[:], xs_tab[:].indirect(offs_t[:]))
         place_rows(xs, xs_rows, X_ROW)
-        rr_raw = [load_rows("rr_raw0", rr, 0, S // 2, "xs_tab")]
+        xw_tab = load_words("xw_tab", x_words, T, "xs_tab")
         pq_rows = new("pq_rows", [P, 2 * V], U8)
         nc.vector.tensor_copy(pq_rows[:, 0:V], ps_tab[:].indirect(tail_t[:]))
-        w2_raw = [load_rows("w2_raw0", w2, 0, W2_CUTS[1], "ps_tab")]
+        qw_tab = load_words("qw_tab", q_words, G, "ps_tab")
         nc.vector.tensor_copy(pq_rows[:, V : 2 * V], qs_tab[:].indirect(tail_t[:]))
-        w2_raw.append(load_rows("w2_raw1", w2, W2_CUTS[1], H, "qs_tab"))
         place_rows(pqs, pq_rows, PQ_ROW)
-        pw = gather_words("pw", pw_tab, tail_t)
+        rr_raw = [load_rows("rr_raw0", rr, 0, S // 2, "qs_tab")]
 
         w1_bf = new("w1_bf", [P, PACK * H], BF16)
         nc.scalar.copy(*cast_views(w1_bf, w1_raw, 0, P, "j t"))
+        ri_raw = [load_rows("ri_raw0", ri, 0, S // 2, "w1_raw")]
         w1q = quantize("w1q", w1_bf[:], H)
-        xw = gather_words("xw", xw_tab, offs_t)
-
-        rr_raw.append(load_rows("rr_raw1", rr, S // 2, S, "w1_raw"))
-        ri_raw = [load_rows("ri_raw0", ri, 0, S // 2, "w1_bf")]
-
-        ybank = [project("ybank", w1q, c, "ybank%d" % c) for c in range(2)]
-        qw = gather_words("qw", qw_tab, tail_t, "xw_tab")
-        ri_raw.append(load_rows("ri_raw1", ri, S // 2, S, "qw_tab"))
+        rr_raw.append(load_rows("rr_raw1", rr, S // 2, S, "w1_bf"))
+        pw = gather_words("pw", pw_tab, tail_t)
+        w2_bf = new("w2_bf", [P, PACK * H], BF16)
+        nc.scalar.copy(*cast_views(w2_bf, w2_raw, 0, P, "j t"))
+        w2q = quantize("w2q", w2_bf[:], H)
+        ri_raw.append(load_rows("ri_raw1", ri, S // 2, S, "w2_bf"))
+        xw = gather_words("xw", xw_tab, offs_t, "w2_raw")
+        ybank = [project("ybank", w1q, c, "bank%d" % c) for c in range(2)]
+        ebank = [project("ebank", w2q, c, "bank%d" % (c + 2)) for c in range(2)]
+        ybank.extend(project("ybank", w1q, c, "bank%d" % (c + 2)) for c in range(2, NQ))
+        qw = gather_words("qw", qw_tab, tail_t, "xs_tab")
         z_bf = [new("z_bf%d" % c, [P, TQ * PACK], BF16) for c in range(NQ)]
         g_bf = [new("g_bf%d" % c, [P, TQ * PACK], BF16) for c in range(NQ)]
         sbank = [[] for _ in range(NQ)]
@@ -170,31 +169,22 @@ def tile_picked_zcplx_simple_p_kernel(tc, x_words, x_scales, w1, w2, rr, ri, p_w
                 queue = nc.scalar if (c, v1) == (NQ - 1, V) else nc.sync
                 queue.dma_start(out[c * TQ : (c + 1) * TQ, v0:v1], res[:])
 
-        w2_bf = new("w2_bf", [P, PACK * H], BF16)
-
-        def w2_cast_views(h, c0, c1):
-            dst = w2_bf[:].rearrange("p (t m j) -> p m j t", t=PACK, j=PACK)[:, c0 // PACK : c1 // PACK, :, :]
-            return dst, w2_raw[h][:, :, c0 - W2_CUTS[h] : c1 - W2_CUTS[h]].rearrange("p j (m t) -> p m j t", t=PACK)
-
-        nc.scalar.copy(*w2_cast_views(0, 0, W2_CUTS[1]))
-        nc.scalar.copy(*w2_cast_views(1, W2_CUTS[1], W2_SCALAR_END))
-        for c in range(2):
-            product(z_bf[c][:], ybank[c], rr_raw, c)
-            ybank.append(project("ybank", w1q, c + 2, "ybank%d" % c))
-        open_scores(0, 0, V, "sbank0")
-        nc.vector.tensor_copy(*w2_cast_views(1, W2_SCALAR_END, H))
-        open_scores(1, 0, V, "sbank1")
-        w2q = quantize("w2q", w2_bf[:], H)
-        ebank = [project("ebank", w2q, c, "ebank%d" % c) for c in range(NQ)]
-        product(z_bf[2][:], ybank[2], rr_raw, 2)
-        product(z_bf[3][:], ybank[3], rr_raw, 3)
-        open_scores(2, 0, V, "ybank0")
+        product(z_bf[0][:], ybank[0], rr_raw, 0)
+        ebank.append(project("ebank", w2q, 2, "bank0"))
+        product(z_bf[1][:], ybank[1], rr_raw, 1)
+        ebank.append(project("ebank", w2q, 3, "bank1"))
+        open_scores(0, 0, V, "bank6")
         product(g_bf[0][:], ebank[0], ri_raw, 0)
-        open_scores(3, 0, V // 2, "ybank1")
-        open_scores(3, V // 2, V, "ebank0")
-        for c in range(1, NQ - 1):
-            product(g_bf[c][:], ebank[c], ri_raw, c)
-            finish(c - 1)
+        open_scores(1, 0, V, "bank7")
+        product(g_bf[1][:], ebank[1], ri_raw, 1)
+        finish(0)
+        product(z_bf[2][:], ybank[2], rr_raw, 2)
+        finish(1)
+        product(z_bf[3][:], ybank[3], rr_raw, 3)
+        open_scores(2, 0, V, "bank2")
+        product(g_bf[2][:], ebank[2], ri_raw, 2)
+        open_scores(3, 0, V // 2, "bank3")
+        open_scores(3, V // 2, V, "bank4")
         product(g_bf[3][:], ebank[3], ri_raw, 3, 0, TQ // 2)
         finish(2)
         product(g_bf[3][:], ebank[3], ri_raw, 3, TQ // 2, TQ)

@@ -22,17 +22,20 @@ TQ = 128
 NQ = S // TQ
 QUAD = 32
 SPREAD = 8
-X_ROW = 4
-PQ_ROW = 12
+PLANE_ROW = 12
+W2_SCALAR = 96
 
 
 def tile_picked_zcplx_simple_p_kernel(tc, x_words, x_scales, w1, w2, rr, ri, p_words, p_scales, q_words, q_scales, offs, tail, out):
     nc = tc.nc
     with ExitStack() as ctx:
         keep = ctx.enter_context(tc.tile_pool(name="keep", bufs=1))
+        placed = ctx.enter_context(tc.tile_pool(name="placed", bufs=1))
         psum = ctx.enter_context(tc.psum_pool(name="psum", bufs=1))
 
         def new(name, shape, dtype, tag=None):
+            if isinstance(tag, int):
+                return placed.tile(shape, dtype, name=name, tag=name, align_bytes=64, offset=tag)
             return keep.tile(shape, dtype, name=name, tag=tag or name, align_bytes=64)
 
         def load_scales(table, scales):
@@ -69,10 +72,9 @@ def tile_picked_zcplx_simple_p_kernel(tc, x_words, x_scales, w1, w2, rr, ri, p_w
         nc.gpsimd.memset(warm[:], 0.0)
         warm_out = new("warm_out", [P, 1], F32)
         nc.scalar.activation(warm_out[:], warm[:], SIGMOID)
-        xs = zeroed("xs", S, nc.gpsimd)
-        pqs = zeroed("pqs", 2 * V, nc.gpsimd)
+        planes = zeroed("planes", S + 2 * V, nc.gpsimd)
 
-        w1_raw = new("w1_raw", [P, PACK, H], F32)
+        w1_raw = new("w1_raw", [P, PACK, H], F32, 8192)
         w1_rows = w1.rearrange("(p j) c -> p j c", j=PACK)
         nc.sync.dma_start(w1_raw[:, 0:2, :], w1_rows[:, 0:2, :])
         offs_t = load_list("offs_t", offs)
@@ -81,8 +83,9 @@ def tile_picked_zcplx_simple_p_kernel(tc, x_words, x_scales, w1, w2, rr, ri, p_w
         load_scales(ps_tab, p_scales)
         load_scales(qs_tab, q_scales)
         nc.sync.dma_start(w1_raw[:, 2:PACK, :], w1_rows[:, 2:PACK, :])
-        w2_raw = load_rows("w2_raw", w2, 0, H)
+        w2_raw = load_rows("w2_raw", w2, 0, H, 0)
         pw_tab = load_words("pw_tab", p_words, G)
+        xw_tab = load_words("xw_tab", x_words, T)
 
         def gather_words(name, table, offsets, tag=None):
             picked = new(name, [P, S], U32, tag)
@@ -106,7 +109,7 @@ def tile_picked_zcplx_simple_p_kernel(tc, x_words, x_scales, w1, w2, rr, ri, p_w
             for j in range(PACK):
                 wc = slice(j * P, (j + 1) * P)
                 nc.tensor.matmul_mx(out=bank[:, j, :], lhsT=wq[0][:, wc].bitcast(FP8X4), lhsT_scale=wq[1][:, wc],
-                                    rhs=xw[:, cols].bitcast(FP8X4), rhs_scale=xs[X_ROW:P, cols], start=True, stop=True)
+                                    rhs=xw[c // 2][:, (c % 2) * TQ : (c % 2 + 1) * TQ].bitcast(FP8X4), rhs_scale=planes[PLANE_ROW:P, cols], start=True, stop=True)
             return bank
 
         def product(dst, bank, pieces, c, t0=0, t1=TQ):
@@ -120,32 +123,33 @@ def tile_picked_zcplx_simple_p_kernel(tc, x_words, x_scales, w1, w2, rr, ri, p_w
                 MULT,
             )
 
-        xs_rows = new("xs_rows", [P, S], U8)
-        nc.vector.tensor_copy(xs_rows[:], xs_tab[:].indirect(offs_t[:]))
-        place_rows(xs, xs_rows, X_ROW)
-        xw_tab = load_words("xw_tab", x_words, T, "xs_tab")
-        pq_rows = new("pq_rows", [P, 2 * V], U8)
-        nc.vector.tensor_copy(pq_rows[:, 0:V], ps_tab[:].indirect(tail_t[:]))
-        qw_tab = load_words("qw_tab", q_words, G, "ps_tab")
-        nc.vector.tensor_copy(pq_rows[:, V : 2 * V], qs_tab[:].indirect(tail_t[:]))
-        place_rows(pqs, pq_rows, PQ_ROW)
-        rr_raw = [load_rows("rr_raw0", rr, 0, S // 2, "qs_tab")]
+        rows = new("rows", [P, S + 2 * V], U8)
+        nc.vector.tensor_copy(rows[:, 0:S], xs_tab[:].indirect(offs_t[:]))
+        nc.vector.tensor_copy(rows[:, S : S + V], ps_tab[:].indirect(tail_t[:]))
+        nc.vector.tensor_copy(rows[:, S + V : S + 2 * V], qs_tab[:].indirect(tail_t[:]))
+        place_rows(planes, rows, PLANE_ROW)
+        qw_tab = load_words("qw_tab", q_words, G, "qs_tab")
 
         w1_bf = new("w1_bf", [P, PACK * H], BF16)
         nc.scalar.copy(*cast_views(w1_bf, w1_raw, 0, P, "j t"))
-        ri_raw = [load_rows("ri_raw0", ri, 0, S // 2, "w1_raw")]
+        rr_raw = [load_rows("rr_raw0", rr, 0, S // 2, 8192)]
+        ri_raw = [load_rows("ri_raw0", ri, 0, S // 2, 12288)]
         w1q = quantize("w1q", w1_bf[:], H)
         rr_raw.append(load_rows("rr_raw1", rr, S // 2, S, "w1_bf"))
-        pw = gather_words("pw", pw_tab, tail_t)
         w2_bf = new("w2_bf", [P, PACK * H], BF16)
-        nc.scalar.copy(*cast_views(w2_bf, w2_raw, 0, P, "j t"))
+        nc.scalar.copy(*cast_views(w2_bf, w2_raw, 0, W2_SCALAR, "j t"))
+        nc.vector.tensor_copy(*cast_views(w2_bf, w2_raw, W2_SCALAR, P, "j t"))
+        pw = gather_words("pw", pw_tab, tail_t)
         w2q = quantize("w2q", w2_bf[:], H)
-        ri_raw.append(load_rows("ri_raw1", ri, S // 2, S, "w2_bf"))
-        xw = gather_words("xw", xw_tab, offs_t, "w2_raw")
+        ri_raw.append(load_rows("ri_raw1", ri, S // 2, S, 0))
+        xw = []
+        for h in range(2):
+            xw.append(new("xw%d" % h, [P, S // 2], U32, 4096 + 1024 * h))
+            nc.vector.tensor_copy(xw[h][:], xw_tab[:].bitcast(U32).indirect(offs_t[:, 16 * h : 16 * (h + 1)]))
         ybank = [project("ybank", w1q, c, "bank%d" % c) for c in range(2)]
         ebank = [project("ebank", w2q, c, "bank%d" % (c + 2)) for c in range(2)]
         ybank.extend(project("ybank", w1q, c, "bank%d" % (c + 2)) for c in range(2, NQ))
-        qw = gather_words("qw", qw_tab, tail_t, "xs_tab")
+        qw = gather_words("qw", qw_tab, tail_t, "w2_bf")
         z_bf = [new("z_bf%d" % c, [P, TQ * PACK], BF16) for c in range(NQ)]
         g_bf = [new("g_bf%d" % c, [P, TQ * PACK], BF16) for c in range(NQ)]
         sbank = [[] for _ in range(NQ)]
@@ -156,14 +160,14 @@ def tile_picked_zcplx_simple_p_kernel(tc, x_words, x_scales, w1, w2, rr, ri, p_w
                 zq[c] = quantize("zq%d" % c, z_bf[c][:], TQ)
             bank = psum.tile([P, v1 - v0], F32, name="sbank%d_%d" % (c, v0), tag=tag)
             nc.tensor.matmul_mx(out=bank[:], lhsT=zq[c][0][:].bitcast(FP8X4), lhsT_scale=zq[c][1][:],
-                                rhs=pw[:, v0:v1].bitcast(FP8X4), rhs_scale=pqs[PQ_ROW:P, v0:v1], start=True, stop=False)
+                                rhs=pw[:, v0:v1].bitcast(FP8X4), rhs_scale=planes[PLANE_ROW:P, S + v0 : S + v1], start=True, stop=False)
             sbank[c].append((bank, v0, v1))
 
         def finish(c):
             gq = quantize("gq%d" % c, g_bf[c][:], TQ)
             for bank, v0, v1 in sbank[c]:
                 nc.tensor.matmul_mx(out=bank[:], lhsT=gq[0][:].bitcast(FP8X4), lhsT_scale=gq[1][:],
-                                    rhs=qw[:, v0:v1].bitcast(FP8X4), rhs_scale=pqs[PQ_ROW:P, V + v0 : V + v1], start=False, stop=True)
+                                    rhs=qw[:, v0:v1].bitcast(FP8X4), rhs_scale=planes[PLANE_ROW:P, S + V + v0 : S + V + v1], start=False, stop=True)
                 res = new("res%d_%d" % (c, v0), [P, v1 - v0], F32)
                 nc.scalar.activation(res[:], bank[:], SIGMOID)
                 queue = nc.scalar if (c, v1) == (NQ - 1, V) else nc.sync
@@ -183,9 +187,9 @@ def tile_picked_zcplx_simple_p_kernel(tc, x_words, x_scales, w1, w2, rr, ri, p_w
         product(z_bf[3][:], ybank[3], rr_raw, 3)
         open_scores(2, 0, V, "bank2")
         product(g_bf[2][:], ebank[2], ri_raw, 2)
-        open_scores(3, 0, V // 2, "bank3")
-        open_scores(3, V // 2, V, "bank4")
         product(g_bf[3][:], ebank[3], ri_raw, 3, 0, TQ // 2)
         finish(2)
         product(g_bf[3][:], ebank[3], ri_raw, 3, TQ // 2, TQ)
+        open_scores(3, 0, V // 2, "bank3")
+        open_scores(3, V // 2, V, "bank4")
         finish(3)

@@ -51,8 +51,8 @@ def tile_picked_zcplx_simple_p_kernel(tc, x_words, x_scales, w1, w2, rr, ri, p_w
             nc.sync.dma_start(raw[:], src.rearrange("(p j) c -> p j c", j=PACK)[:, :, c0:c1])
             return raw
 
-        def zeroed(name, width, engine):
-            table = new(name, [P, width], U8)
+        def zeroed(name, width, engine, tag=None):
+            table = new(name, [P, width], U8, tag)
             engine.memset(table[:].bitcast(I32), 0)
             return table
 
@@ -72,7 +72,7 @@ def tile_picked_zcplx_simple_p_kernel(tc, x_words, x_scales, w1, w2, rr, ri, p_w
         nc.gpsimd.memset(warm[:], 0.0)
         warm_out = new("warm_out", [P, 1], F32)
         nc.scalar.activation(warm_out[:], warm[:], SIGMOID)
-        planes = zeroed("planes", S + 2 * V, nc.gpsimd)
+        x_plane = zeroed("x_plane", S, nc.gpsimd)
 
         w1_raw = new("w1_raw", [P, PACK, H], F32, 8192)
         w1_rows = w1.rearrange("(p j) c -> p j c", j=PACK)
@@ -109,7 +109,7 @@ def tile_picked_zcplx_simple_p_kernel(tc, x_words, x_scales, w1, w2, rr, ri, p_w
             for j in range(PACK):
                 wc = slice(j * P, (j + 1) * P)
                 nc.tensor.matmul_mx(out=bank[:, j, :], lhsT=wq[0][:, wc].bitcast(FP8X4), lhsT_scale=wq[1][:, wc],
-                                    rhs=xw[c // 2][:, (c % 2) * TQ : (c % 2 + 1) * TQ].bitcast(FP8X4), rhs_scale=planes[PLANE_ROW:P, cols], start=True, stop=True)
+                                    rhs=xw[c // 2][:, (c % 2) * TQ : (c % 2 + 1) * TQ].bitcast(FP8X4), rhs_scale=x_plane[PLANE_ROW:P, cols], start=True, stop=True)
             return bank
 
         def product(dst, bank, pieces, c, t0=0, t1=TQ):
@@ -123,25 +123,28 @@ def tile_picked_zcplx_simple_p_kernel(tc, x_words, x_scales, w1, w2, rr, ri, p_w
                 MULT,
             )
 
-        rows = new("rows", [P, S + 2 * V], U8)
-        nc.vector.tensor_copy(rows[:, 0:S], xs_tab[:].indirect(offs_t[:]))
-        nc.vector.tensor_copy(rows[:, S : S + V], ps_tab[:].indirect(tail_t[:]))
-        nc.vector.tensor_copy(rows[:, S + V : S + 2 * V], qs_tab[:].indirect(tail_t[:]))
-        place_rows(planes, rows, PLANE_ROW)
-        qw_tab = load_words("qw_tab", q_words, G, "qs_tab")
+        x_rows = new("x_rows", [P, S], U8)
+        nc.vector.tensor_copy(x_rows[:], xs_tab[:].indirect(offs_t[:]))
+        pq_rows = new("pq_rows", [P, 2 * V], U8)
+        nc.vector.tensor_copy(pq_rows[:, 0:V], ps_tab[:].indirect(tail_t[:]))
+        nc.vector.tensor_copy(pq_rows[:, V : 2 * V], qs_tab[:].indirect(tail_t[:]))
+        place_rows(x_plane, x_rows, PLANE_ROW)
+        qw_tab = load_words("qw_tab", q_words, G, "xs_tab")
 
         w1_bf = new("w1_bf", [P, PACK * H], BF16)
         nc.scalar.copy(*cast_views(w1_bf, w1_raw, 0, P, "j t"))
         rr_raw = [load_rows("rr_raw0", rr, 0, S // 2, 8192)]
-        ri_raw = [load_rows("ri_raw0", ri, 0, S // 2, 12288)]
+        pq_plane = zeroed("pq_plane", 2 * V, nc.gpsimd, 12288)
+        place_rows(pq_plane, pq_rows, PLANE_ROW)
         w1q = quantize("w1q", w1_bf[:], H)
-        rr_raw.append(load_rows("rr_raw1", rr, S // 2, S, "w1_bf"))
+        ri_raw = [load_rows("ri_raw0", ri, 0, S // 2, "w1_bf")]
         w2_bf = new("w2_bf", [P, PACK * H], BF16)
         nc.scalar.copy(*cast_views(w2_bf, w2_raw, 0, W2_SCALAR, "j t"))
         nc.vector.tensor_copy(*cast_views(w2_bf, w2_raw, W2_SCALAR, P, "j t"))
         pw = gather_words("pw", pw_tab, tail_t)
         w2q = quantize("w2q", w2_bf[:], H)
-        ri_raw.append(load_rows("ri_raw1", ri, S // 2, S, 0))
+        rr_raw.append(load_rows("rr_raw1", rr, S // 2, S, 0))
+        ri_raw.append(load_rows("ri_raw1", ri, S // 2, S, "w2_bf"))
         xw = []
         for h in range(2):
             xw.append(new("xw%d" % h, [P, S // 2], U32, 4096 + 1024 * h))
@@ -149,7 +152,7 @@ def tile_picked_zcplx_simple_p_kernel(tc, x_words, x_scales, w1, w2, rr, ri, p_w
         ybank = [project("ybank", w1q, c, "bank%d" % c) for c in range(2)]
         ebank = [project("ebank", w2q, c, "bank%d" % (c + 2)) for c in range(2)]
         ybank.extend(project("ybank", w1q, c, "bank%d" % (c + 2)) for c in range(2, NQ))
-        qw = gather_words("qw", qw_tab, tail_t, "w2_bf")
+        qw = gather_words("qw", qw_tab, tail_t, 6144)
         z_bf = [new("z_bf%d" % c, [P, TQ * PACK], BF16) for c in range(NQ)]
         g_bf = [new("g_bf%d" % c, [P, TQ * PACK], BF16) for c in range(NQ)]
         sbank = [[] for _ in range(NQ)]
@@ -160,14 +163,14 @@ def tile_picked_zcplx_simple_p_kernel(tc, x_words, x_scales, w1, w2, rr, ri, p_w
                 zq[c] = quantize("zq%d" % c, z_bf[c][:], TQ)
             bank = psum.tile([P, v1 - v0], F32, name="sbank%d_%d" % (c, v0), tag=tag)
             nc.tensor.matmul_mx(out=bank[:], lhsT=zq[c][0][:].bitcast(FP8X4), lhsT_scale=zq[c][1][:],
-                                rhs=pw[:, v0:v1].bitcast(FP8X4), rhs_scale=planes[PLANE_ROW:P, S + v0 : S + v1], start=True, stop=False)
+                                rhs=pw[:, v0:v1].bitcast(FP8X4), rhs_scale=pq_plane[PLANE_ROW:P, v0:v1], start=True, stop=False)
             sbank[c].append((bank, v0, v1))
 
         def finish(c):
             gq = quantize("gq%d" % c, g_bf[c][:], TQ)
             for bank, v0, v1 in sbank[c]:
                 nc.tensor.matmul_mx(out=bank[:], lhsT=gq[0][:].bitcast(FP8X4), lhsT_scale=gq[1][:],
-                                    rhs=qw[:, v0:v1].bitcast(FP8X4), rhs_scale=planes[PLANE_ROW:P, S + V + v0 : S + V + v1], start=False, stop=True)
+                                    rhs=qw[:, v0:v1].bitcast(FP8X4), rhs_scale=pq_plane[PLANE_ROW:P, V + v0 : V + v1], start=False, stop=True)
                 res = new("res%d_%d" % (c, v0), [P, v1 - v0], F32)
                 nc.scalar.activation(res[:], bank[:], SIGMOID)
                 queue = nc.scalar if (c, v1) == (NQ - 1, V) else nc.sync

@@ -23,6 +23,7 @@ NQ = S // TQ
 QUAD = 32
 SPREAD = 8
 PLANE_ROW = 12
+PQ_ROW = 4
 W2_SCALAR = 96
 
 
@@ -38,8 +39,8 @@ def tile_picked_zcplx_simple_p_kernel(tc, x_words, x_scales, w1, w2, rr, ri, p_w
                 return placed.tile(shape, dtype, name=name, tag=name, align_bytes=64, offset=tag)
             return keep.tile(shape, dtype, name=name, tag=tag or name, align_bytes=64)
 
-        def load_scales(table, scales):
-            nc.sync.dma_start(table[0:P:SPREAD, :].bitcast(I32), scales[0].bitcast(I32))
+        def load_scales(table, scales, first):
+            nc.sync.dma_start(table[first:P:SPREAD, :].bitcast(I32), scales[0].bitcast(I32))
 
         def load_words(name, words, width, tag=None):
             table = new(name, [P, width], I32, tag)
@@ -63,7 +64,7 @@ def tile_picked_zcplx_simple_p_kernel(tc, x_words, x_scales, w1, w2, rr, ri, p_w
 
         def place_rows(plane, rows, first):
             for r in range(4):
-                nc.sync.dma_start(plane[first + r : P : QUAD, :].bitcast(I32), rows[SPREAD * r : P : QUAD, :].bitcast(I32))
+                nc.sync.dma_start(plane[PLANE_ROW + r : P : QUAD, :].bitcast(I32), rows[first + SPREAD * r : P : QUAD, :].bitcast(I32))
 
         xs_tab = zeroed("xs_tab", T, nc.gpsimd)
         ps_tab = zeroed("ps_tab", G, nc.vector)
@@ -78,10 +79,10 @@ def tile_picked_zcplx_simple_p_kernel(tc, x_words, x_scales, w1, w2, rr, ri, p_w
         w1_rows = w1.rearrange("(p j) c -> p j c", j=PACK)
         nc.sync.dma_start(w1_raw[:, 0:2, :], w1_rows[:, 0:2, :])
         offs_t = load_list("offs_t", offs)
-        load_scales(xs_tab, x_scales)
+        load_scales(xs_tab, x_scales, 0)
         tail_t = load_list("tail_t", tail)
-        load_scales(ps_tab, p_scales)
-        load_scales(qs_tab, q_scales)
+        load_scales(ps_tab, p_scales, PQ_ROW)
+        load_scales(qs_tab, q_scales, PQ_ROW)
         nc.sync.dma_start(w1_raw[:, 2:PACK, :], w1_rows[:, 2:PACK, :])
         w2_raw = load_rows("w2_raw", w2, 0, H, 0)
         pw_tab = load_words("pw_tab", p_words, G)
@@ -128,16 +129,16 @@ def tile_picked_zcplx_simple_p_kernel(tc, x_words, x_scales, w1, w2, rr, ri, p_w
         pq_rows = new("pq_rows", [P, 2 * V], U8)
         nc.vector.tensor_copy(pq_rows[:, 0:V], ps_tab[:].indirect(tail_t[:]))
         nc.vector.tensor_copy(pq_rows[:, V : 2 * V], qs_tab[:].indirect(tail_t[:]))
-        place_rows(x_plane, x_rows, PLANE_ROW)
+        place_rows(x_plane, x_rows, 0)
         qw_tab = load_words("qw_tab", q_words, G, "xs_tab")
 
         w1_bf = new("w1_bf", [P, PACK * H], BF16)
         nc.scalar.copy(*cast_views(w1_bf, w1_raw, 0, P, "j t"))
         rr_raw = [load_rows("rr_raw0", rr, 0, S // 2, 8192)]
-        pq_plane = zeroed("pq_plane", 2 * V, nc.gpsimd, 12288)
-        place_rows(pq_plane, pq_rows, PLANE_ROW)
+        ri_raw = [load_rows("ri_raw0", ri, 0, S // 2, 12288)]
         w1q = quantize("w1q", w1_bf[:], H)
-        ri_raw = [load_rows("ri_raw0", ri, 0, S // 2, "w1_bf")]
+        pq_plane = zeroed("pq_plane", 2 * V, nc.gpsimd, "w1_bf")
+        place_rows(pq_plane, pq_rows, PQ_ROW)
         w2_bf = new("w2_bf", [P, PACK * H], BF16)
         nc.scalar.copy(*cast_views(w2_bf, w2_raw, 0, W2_SCALAR, "j t"))
         nc.vector.tensor_copy(*cast_views(w2_bf, w2_raw, W2_SCALAR, P, "j t"))

@@ -137,7 +137,7 @@ def tile_picked_zcplx_simple_p_kernel(tc, x_words, x_scales, w1, w2, rr, ri, p_w
         rr_raw = [load_rows("rr_raw0", rr, 0, S // 2, 8192)]
         ri_raw = [load_rows("ri_raw0", ri, 0, S // 2, 12288)]
         w1q = quantize("w1q", w1_bf[:], H)
-        pq_plane = zeroed("pq_plane", 2 * V, nc.gpsimd, "w1_bf")
+        pq_plane = new("pq_plane", [P, 2 * V], U8, "w1_bf")
         place_rows(pq_plane, pq_rows, PQ_ROW)
         w2_bf = new("w2_bf", [P, PACK * H], BF16)
         nc.scalar.copy(*cast_views(w2_bf, w2_raw, 0, W2_SCALAR, "j t"))

@@ -135,10 +135,10 @@ def tile_picked_zcplx_simple_p_kernel(tc, x_words, x_scales, w1, w2, rr, ri, p_w
         w1_bf = new("w1_bf", [P, PACK * H], BF16)
         nc.scalar.copy(*cast_views(w1_bf, w1_raw, 0, P, "j t"))
         rr_raw = [load_rows("rr_raw0", rr, 0, S // 2, 8192)]
-        ri_raw = [load_rows("ri_raw0", ri, 0, S // 2, 12288)]
-        w1q = quantize("w1q", w1_bf[:], H)
-        pq_plane = new("pq_plane", [P, 2 * V], U8, "w1_bf")
+        pq_plane = new("pq_plane", [P, 2 * V], U8, 12288)
         place_rows(pq_plane, pq_rows, PQ_ROW)
+        w1q = quantize("w1q", w1_bf[:], H)
+        ri_raw = [load_rows("ri_raw0", ri, 0, S // 2, "w1_bf")]
         w2_bf = new("w2_bf", [P, PACK * H], BF16)
         nc.scalar.copy(*cast_views(w2_bf, w2_raw, 0, W2_SCALAR, "j t"))
         nc.vector.tensor_copy(*cast_views(w2_bf, w2_raw, W2_SCALAR, P, "j t"))

from contextlib import ExitStack

import concourse.mybir as mybir

K, T, S, V, H, G = 512, 2048, 512, 512, 512, 1024
FLOPS = 2 * 2 * K * H * S + 2 * 2 * H * S * V

F32 = mybir.dt.float32
BF16 = mybir.dt.bfloat16
I32 = mybir.dt.int32
U32 = mybir.dt.uint32
U16 = mybir.dt.uint16
U8 = mybir.dt.uint8
FP8X4 = mybir.dt.float8_e4m3fn_x4
MULT = mybir.AluOpType.mult
ADD = mybir.AluOpType.add
SIGMOID = mybir.ActivationFunctionType.Sigmoid

P = 128
PACK = 4
TQ = 128
NQ = S // TQ
QUAD = 32
SPREAD = 8
PLANE_ROW = 12
PQ_ROW = 4
W2_SCALAR = 96


def tile_picked_zcplx_simple_p_kernel(tc, x_words, x_scales, w1, w2, rr, ri, p_words, p_scales, q_words, q_scales, offs, tail, out):
    nc = tc.nc
    with ExitStack() as ctx:
        keep = ctx.enter_context(tc.tile_pool(name="keep", bufs=1))
        placed = ctx.enter_context(tc.tile_pool(name="placed", bufs=1))
        psum = ctx.enter_context(tc.psum_pool(name="psum", bufs=1))

        def new(name, shape, dtype, tag=None):
            if isinstance(tag, int):
                return placed.tile(shape, dtype, name=name, tag=name, align_bytes=64, offset=tag)
            return keep.tile(shape, dtype, name=name, tag=tag or name, align_bytes=64)

        def load_scales(table, scales, first):
            nc.sync.dma_start(table[first:P:SPREAD, :].bitcast(I32), scales[0].bitcast(I32))

        def load_words(name, words, width, tag=None):
            table = new(name, [P, width], I32, tag)
            nc.sync.dma_start(table[:], words[0].rearrange("p n t -> p (n t)").bitcast(I32))
            return table

        def load_rows(name, src, c0, c1, tag=None):
            raw = new(name, [P, PACK, c1 - c0], F32, tag)
            nc.sync.dma_start(raw[:], src.rearrange("(p j) c -> p j c", j=PACK)[:, :, c0:c1])
            return raw

        def zeroed(name, width, engine, tag=None):
            table = new(name, [P, width], U8, tag)
            engine.memset(table[:].bitcast(I32), 0)
            return table

        def load_list(name, src):
            tile = new(name, [P, S // 16], U16)
            nc.sync.dma_start(tile[:], src)
            return tile

        def place_rows(plane, rows, first):
            for r in range(4):
                nc.sync.dma_start(plane[PLANE_ROW + r : P : QUAD, :].bitcast(I32), rows[first + SPREAD * r : P : QUAD, :].bitcast(I32))

        xs_tab = zeroed("xs_tab", T, nc.gpsimd)
        ps_tab = zeroed("ps_tab", G, nc.vector)
        qs_tab = zeroed("qs_tab", G, nc.vector)
        warm = new("warm", [P, 1], F32)
        nc.gpsimd.memset(warm[:], 0.0)
        warm_out = new("warm_out", [P, 1], F32)
        nc.scalar.activation(warm_out[:], warm[:], SIGMOID)
        x_plane = zeroed("x_plane", S, nc.gpsimd)

        w1_raw = new("w1_raw", [P, PACK, H], F32, 8192)
        w1_rows = w1.rearrange("(p j) c -> p j c", j=PACK)
        nc.sync.dma_start(w1_raw[:, 0:2, :], w1_rows[:, 0:2, :])
        offs_t = load_list("offs_t", offs)
        load_scales(xs_tab, x_scales, 0)
        tail_t = load_list("tail_t", tail)
        load_scales(ps_tab, p_scales, PQ_ROW)
        load_scales(qs_tab, q_scales, PQ_ROW)
        nc.sync.dma_start(w1_raw[:, 2:PACK, :], w1_rows[:, 2:PACK, :])
        w2_raw = load_rows("w2_raw", w2, 0, H, 0)
        pw_tab = load_words("pw_tab", p_words, G)
        xw_tab = load_words("xw_tab", x_words, T)

        def gather_words(name, table, offsets, tag=None):
            picked = new(name, [P, S], U32, tag)
            nc.vector.tensor_copy(picked[:], table[:].bitcast(U32).indirect(offsets[:]))
            return picked

        def cast_views(grouped, raw, m0, m1, order):
            dst = grouped[:].rearrange("p (t m j) -> p m %s" % order, t=PACK, j=PACK)
            src = raw[:].rearrange("p j (m t) -> p m %s" % order, t=PACK)
            return dst[:, m0:m1, :, :], src[:, m0:m1, :, :]

        def quantize(name, grouped, width, tag=None):
            codes = new(name + "_codes", [P, width], U32, tag)
            scales = new(name + "_scales", [P, width], U8)
            nc.vector.quantize_mx(out=codes[:].bitcast(FP8X4), scales=scales[:], in_=grouped)
            return codes, scales

        def project(name, wq, c, tag):
            bank = psum.tile([P, PACK, TQ], F32, name="%s%d" % (name, c), tag=tag)
            cols = slice(c * TQ, (c + 1) * TQ)
            for j in range(PACK):
                wc = slice(j * P, (j + 1) * P)
                nc.tensor.matmul_mx(out=bank[:, j, :], lhsT=wq[0][:, wc].bitcast(FP8X4), lhsT_scale=wq[1][:, wc],
                                    rhs=xw[c // 2][:, (c % 2) * TQ : (c % 2 + 1) * TQ].bitcast(FP8X4), rhs_scale=x_plane[PLANE_ROW:P, cols], start=True, stop=True)
            return bank

        def product(dst, bank, pieces, c, t0=0, t1=TQ):
            per = NQ // len(pieces)
            raw = pieces[c // per]
            c0 = (c % per) * TQ
            nc.vector.tensor_tensor(
                dst[:, t0 * PACK : t1 * PACK].rearrange("p (c i j) -> p c j i", i=2, j=PACK),
                bank[:, :, t0:t1].rearrange("p j (c i) -> p c j i", i=2),
                raw[:, :, c0 + t0 : c0 + t1].rearrange("p j (c i) -> p c j i", i=2),
                MULT,
            )

        x_rows = new("x_rows", [P, S], U8)
        nc.vector.tensor_copy(x_rows[:], xs_tab[:].indirect(offs_t[:]))
        pq_rows = new("pq_rows", [P, 2 * V], U8)
        nc.vector.tensor_copy(pq_rows[:, 0:V], ps_tab[:].indirect(tail_t[:]))
        nc.vector.tensor_copy(pq_rows[:, V : 2 * V], qs_tab[:].indirect(tail_t[:]))
        place_rows(x_plane, x_rows, 0)
        qw_tab = load_words("qw_tab", q_words, G, "xs_tab")

        w1_bf = new("w1_bf", [P, PACK * H], BF16)
        nc.scalar.copy(*cast_views(w1_bf, w1_raw, 0, P, "j t"))
        rr_raw = [load_rows("rr_raw0", rr, 0, S // 2, 8192)]
        pq_plane = new("pq_plane", [P, 2 * V], U8, 12288)
        place_rows(pq_plane, pq_rows, PQ_ROW)
        w1q = quantize("w1q", w1_bf[:], H)
        ri_raw = [load_rows("ri_raw0", ri, 0, S // 2, "w1_bf")]
        w2_bf = new("w2_bf", [P, PACK * H], BF16)
        nc.scalar.copy(*cast_views(w2_bf, w2_raw, 0, W2_SCALAR, "j t"))
        nc.vector.tensor_copy(*cast_views(w2_bf, w2_raw, W2_SCALAR, P, "j t"))
        pw = gather_words("pw", pw_tab, tail_t)
        w2q = quantize("w2q", w2_bf[:], H)
        rr_raw.append(load_rows("rr_raw1", rr, S // 2, S, 0))
        ri_raw.append(load_rows("ri_raw1", ri, S // 2, S, "w2_bf"))
        xw = []
        for h in range(2):
            xw.append(new("xw%d" % h, [P, S // 2], U32, 4096 + 1024 * h))
            nc.vector.tensor_copy(xw[h][:], xw_tab[:].bitcast(U32).indirect(offs_t[:, 16 * h : 16 * (h + 1)]))
        ybank = [project("ybank", w1q, c, "bank%d" % c) for c in range(2)]
        ebank = [project("ebank", w2q, c, "bank%d" % (c + 2)) for c in range(2)]
        ybank.extend(project("ybank", w1q, c, "bank%d" % (c + 2)) for c in range(2, NQ))
        qw = gather_words("qw", qw_tab, tail_t, 6144)
        z_bf = [new("z_bf%d" % c, [P, TQ * PACK], BF16) for c in range(NQ)]
        g_bf = [new("g_bf%d" % c, [P, TQ * PACK], BF16) for c in range(NQ)]
        sbank = [[] for _ in range(NQ)]
        zq = {}

        def open_scores(c, v0, v1, tag):
            if c not in zq:
                zq[c] = quantize("zq%d" % c, z_bf[c][:], TQ)
            bank = psum.tile([P, v1 - v0], F32, name="sbank%d_%d" % (c, v0), tag=tag)
            nc.tensor.matmul_mx(out=bank[:], lhsT=zq[c][0][:].bitcast(FP8X4), lhsT_scale=zq[c][1][:],
                                rhs=pw[:, v0:v1].bitcast(FP8X4), rhs_scale=pq_plane[PLANE_ROW:P, v0:v1], start=True, stop=False)
            sbank[c].append((bank, v0, v1))

        def finish(c):
            gq = quantize("gq%d" % c, g_bf[c][:], TQ)
            for bank, v0, v1 in sbank[c]:
                nc.tensor.matmul_mx(out=bank[:], lhsT=gq[0][:].bitcast(FP8X4), lhsT_scale=gq[1][:],
                                    rhs=qw[:, v0:v1].bitcast(FP8X4), rhs_scale=pq_plane[PLANE_ROW:P, V + v0 : V + v1], start=False, stop=True)
                res = new("res%d_%d" % (c, v0), [P, v1 - v0], F32)
                nc.scalar.activation(res[:], bank[:], SIGMOID)
                queue = nc.scalar if (c, v1) == (NQ - 1, V) else nc.sync
                queue.dma_start(out[c * TQ : (c + 1) * TQ, v0:v1], res[:])

        product(z_bf[0][:], ybank[0], rr_raw, 0)
        ebank.append(project("ebank", w2q, 2, "bank0"))
        product(z_bf[1][:], ybank[1], rr_raw, 1)
        ebank.append(project("ebank", w2q, 3, "bank1"))
        open_scores(0, 0, V, "bank6")
        product(g_bf[0][:], ebank[0], ri_raw, 0)
        open_scores(1, 0, V, "bank7")
        product(g_bf[1][:], ebank[1], ri_raw, 1)
        finish(0)
        product(z_bf[2][:], ybank[2], rr_raw, 2)
        finish(1)
        product(z_bf[3][:], ybank[3], rr_raw, 3)
        open_scores(2, 0, V, "bank2")
        product(g_bf[2][:], ebank[2], ri_raw, 2)
        product(g_bf[3][:], ebank[3], ri_raw, 3, 0, TQ // 2)
        finish(2)
        product(g_bf[3][:], ebank[3], ri_raw, 3, TQ // 2, TQ)
        open_scores(3, 0, V // 2, "bank3")
        open_scores(3, V // 2, V, "bank4")
        finish(3)
